import numpy as np
import ml_dtypes


def mxq(x, axis, fmt="e4m3"):
    dtype, down = {"e4m3": (ml_dtypes.float8_e4m3fn, 7), "e5m2": (ml_dtypes.float8_e5m2, 14)}[fmt]
    v = np.moveaxis(np.asarray(x, np.float32).astype(ml_dtypes.bfloat16).astype(np.float64), axis, -1)
    blocks = v.reshape(v.shape[:-1] + (-1, 32))
    amax = np.abs(blocks).max(-1, keepdims=True)
    byte = np.maximum(np.where(amax > 0, np.frexp(amax)[1] - 1 + 127, 0) - down, 1)
    scale = np.exp2(byte - 127.0)
    codes = (blocks / scale).astype(np.float32).astype(dtype).astype(np.float64)
    return np.moveaxis((codes * scale).reshape(v.shape), -1, axis)


WIDE = False


def mx_kscale(k):
    if not WIDE:
        return np.ones(k)
    levels = np.array([10, -10, 5, -5, 0])
    if k % 512:
        return np.exp2(np.random.permutation(np.resize(levels, k // 32))).repeat(32)
    a = np.empty((k // 512, 16))
    for p in range(k // 512):
        a[p, :8] = np.random.permutation(np.resize(levels, 8))
        for g in range(8):
            far = levels[np.abs(levels - a[p, g]) >= 10]
            a[p, g + 8] = far[np.random.randint(len(far))]
    return np.exp2(a.ravel()).repeat(32)


def f64(x):
    return np.asarray(x).astype(np.float64)


def striped(idx):
    return np.tile(idx.reshape(-1, 16).T, (8, 1)).astype(np.uint16)


def unstriped(offs):
    return offs[:16].T.reshape(-1).astype(np.int64)


def silu(v):
    return v / (1.0 + np.exp(-np.maximum(v, -700.0)))


K, T, E, C, H, N = 1024, 768, 6, 128, 1024, 256


def by_expert(wq, xq):
    return np.concatenate([wq[e].T @ xq[:, e * C:(e + 1) * C] for e in range(E)], axis=1)


def setup_inputs():
    n = np.random.standard_normal
    s = mx_kscale(K)[:, None]
    u = mx_kscale(H)
    return {
        "xT": (n((K, T)) * s).astype(np.float32),
        "w1": (n((E, K, H)) / np.sqrt(K) / s[None] * u[None, None, :]).astype(np.float32),
        "w2": (n((E, H, N)) / np.sqrt(H) / u[None, :, None]).astype(np.float32),
        "gate": np.tile(np.random.uniform(0.2, 1.0, E * C), (N, 1)).astype(np.float32),
        "offs": striped(np.random.permutation(T)[:E * C]),
    }


def reference(xT, w1, w2, gate, offs):
    idx = unstriped(offs)
    xq = mxq(f64(xT)[:, idx], 0, "e4m3")
    h = silu(by_expert(mxq(f64(w1), 1, "e4m3"), xq))
    y = by_expert(mxq(f64(w2), 1, "e4m3"), mxq(h, 0, "e4m3"))
    out = np.zeros((N, T))
    out[:, idx] = f64(gate) * y
    return out

@@ -1,0 +1,190 @@
+from contextlib import ExitStack
+
+import concourse.mybir as mybir
+
+K, T, E, C, H, N = 1024, 768, 6, 128, 1024, 256
+FLOPS = 2 * K * H * E * C + 2 * H * N * E * C
+
+F32 = mybir.dt.float32
+BF16 = mybir.dt.bfloat16
+U32 = mybir.dt.uint32
+U16 = mybir.dt.uint16
+U8 = mybir.dt.uint8
+FP8X4 = mybir.dt.float8_e4m3fn_x4
+MULT = mybir.AluOpType.mult
+SILU = mybir.ActivationFunctionType.Silu
+
+P = 128
+PACK = 4
+PASS = P * PACK
+G = K // PASS
+HB = H // PASS
+NB = N // P
+
+
+def tile_routed_moe_kernel(tc, xT, w1, w2, gate, offs, out):
+    nc = tc.nc
+    xT_v = xT.rearrange("(g p j) t -> g p j t", p=P, j=PACK)
+    w1_v = w1.rearrange("e (g p j) c -> e g p j c", p=P, j=PACK)
+    w2_v = w2.rearrange("e (g p j) c -> e g p j c", p=P, j=PACK)
+    out_v = out.rearrange("(b p) t -> b p t", p=P)
+
+    with ExitStack() as ctx:
+        keep = ctx.enter_context(tc.tile_pool(name="keep", bufs=1))
+        raws = ctx.enter_context(tc.tile_pool(name="raws", bufs=6))
+        raws2 = ctx.enter_context(tc.tile_pool(name="raws2", bufs=4))
+        grp = ctx.enter_context(tc.tile_pool(name="grp", bufs=3))
+        cod = ctx.enter_context(tc.tile_pool(name="cod", bufs=8))
+        hid = ctx.enter_context(tc.tile_pool(name="hid", bufs=3))
+        psum_a = ctx.enter_context(tc.psum_pool(name="psum_a", bufs=4))
+        psum_y = ctx.enter_context(tc.psum_pool(name="psum_y", bufs=2))
+
+        warm_in = keep.tile([P, 1], F32, name="warm_in")
+        warm_out = keep.tile([P, 1], F32, name="warm_out")
+        nc.vector.memset(warm_in[:], 0.0)
+        nc.scalar.activation(warm_out[:], warm_in[:], SILU)
+
+        offsets = keep.tile([P, E * C // 16], U16, name="offsets")
+        gate_sb = keep.tile([P, NB, E * C], F32, name="gate_sb")
+        xw = [keep.tile([P, T], U32, name=f"xw{g}", align_bytes=64) for g in range(G)]
+        xs = [keep.tile([P, T], U8, name=f"xs{g}", align_bytes=64) for g in range(G)]
+        gw = keep.tile([P, G, E * C], U32, name="gw", align_bytes=64)
+        gs = keep.tile([P, G, E * C], U8, name="gs", align_bytes=64)
+        window = [keep.tile([P, T], F32, name=f"window{b}") for b in range(NB)]
+
+        for g in range(G):
+            nc.gpsimd.memset(xs[g][:], 0)
+
+        for g in range(G):
+            raw = raws.tile([P, PACK, T], F32, name="raw_x", tag="raw")
+            nc.sync.dma_start(out=raw[:], in_=xT_v[g])
+            if g == G - 1:
+                nc.sync.dma_start(offsets[:], offs)
+            for t0, t1, copy in ((0, 512, nc.vector.tensor_copy), (512, 768, nc.scalar.copy)):
+                grouped = grp.tile([P, (t1 - t0) * PACK], BF16, name=f"grp_x{t0}", align_bytes=64)
+                copy(
+                    out=grouped[:].rearrange("p (c i j) -> p c j i", i=4, j=PACK),
+                    in_=raw[:, :, t0:t1].rearrange("p j (c i) -> p c j i", i=4),
+                )
+                nc.vector.quantize_mx(
+                    out=xw[g][:, t0:t1].bitcast(FP8X4), scales=xs[g][:, t0:t1], in_=grouped[:]
+                )
+        half = E * C // 2
+        for s in range(2):
+            for g in range(G):
+                sl = offsets[:, s * half // 16 : (s + 1) * half // 16]
+                nc.vector.tensor_copy(out=gw[:, g, s * half : (s + 1) * half], in_=xw[g][:].indirect(sl))
+                nc.vector.tensor_copy(out=gs[:, g, s * half : (s + 1) * half], in_=xs[g][:].indirect(sl))
+
+        w1q = {}
+        w2q = {}
+
+        def load_w1(e):
+            for g in range(G):
+                raw = raws.tile([P, PACK, H], F32, name="raw_w1", tag="raw")
+                last = e == E - 1 and g == G - 1
+                for c0 in range(0, H, PASS if last else H):
+                    c1 = c0 + (PASS if last else H)
+                    nc.sync.dma_start(out=raw[:, :, c0:c1], in_=w1_v[e, g][:, :, c0:c1])
+                for h in range(HB):
+                    grouped = grp.tile([P, PASS * PACK], BF16, name=f"grp_w1_{h}", align_bytes=64)
+                    dst = grouped[:].rearrange("p (t m j) -> p m j t", t=PACK, j=PACK)
+                    src = raw[:, :, h * PASS : (h + 1) * PASS].rearrange("p j (m t) -> p m j t", t=PACK)
+                    cut = 48 if last else (P if h == 0 else 0)
+                    if cut > 0:
+                        nc.scalar.copy(out=dst[:, :cut], in_=src[:, :cut])
+                    if cut < P:
+                        nc.vector.tensor_copy(out=dst[:, cut:], in_=src[:, cut:])
+                    codes = cod.tile([P, PASS], U32, name="w1_codes", align_bytes=64)
+                    scales = cod.tile([P, PASS], U8, name="w1_scales", align_bytes=64)
+                    nc.vector.quantize_mx(out=codes[:].bitcast(FP8X4), scales=scales[:], in_=grouped[:])
+                    w1q[e, g, h] = (codes, scales)
+
+        def load_w2(e):
+            codes = hid.tile([P, HB, N], U32, name="w2_codes", align_bytes=64)
+            scales = hid.tile([P, HB, N], U8, name="w2_scales", align_bytes=64)
+            for h in range(HB):
+                raw = raws2.tile([P, PACK, N], F32, name="raw_w2")
+                nc.sync.dma_start(out=raw[:], in_=w2_v[e, h])
+                grouped = grp.tile([P, N * PACK], BF16, name="grp_w2", align_bytes=64)
+                dst = grouped[:].rearrange("p (c i j) -> p c j i", i=4, j=PACK)
+                src = raw[:].rearrange("p j (c i) -> p c j i", i=4)
+                cut = 24 if e == E - 1 and h == HB - 1 else N // 4
+                if cut > 0:
+                    nc.scalar.copy(out=dst[:, :cut], in_=src[:, :cut])
+                if cut < N // 4:
+                    nc.vector.tensor_copy(out=dst[:, cut:], in_=src[:, cut:])
+                nc.vector.quantize_mx(out=codes[:, h, :].bitcast(FP8X4), scales=scales[:, h, :], in_=grouped[:])
+            w2q[e] = (codes, scales)
+
+        hq = {}
+
+        def layer1(e):
+            slots = slice(e * C, (e + 1) * C)
+            grouped = hid.tile([P, HB, C * PACK], BF16, name="grp_h", align_bytes=64)
+            for h in range(HB):
+                acc = psum_a.tile([P, PACK, C], F32, name="acc_a")
+                for t in range(PACK):
+                    for g in range(G):
+                        codes, scales = w1q[e, g, h]
+                        nc.tensor.matmul_mx(
+                            out=acc[:, t, :],
+                            lhsT=codes[:, t * P : (t + 1) * P].bitcast(FP8X4),
+                            lhsT_scale=scales[:, t * P : (t + 1) * P],
+                            rhs=gw[:, g, slots].bitcast(FP8X4),
+                            rhs_scale=gs[:, g, slots],
+                            start=(g == 0),
+                            stop=(g == G - 1),
+                        )
+                nc.scalar.activation(
+                    grouped[:, h, :].rearrange("p (n t) -> p n t", t=PACK),
+                    acc[:].rearrange("p t n -> p n t"),
+                    SILU,
+                )
+            codes = hid.tile([P, HB, C], U32, name="h_codes", align_bytes=64)
+            scales = hid.tile([P, HB, C], U8, name="h_scales", align_bytes=64)
+            nc.vector.quantize_mx(
+                out=codes[:].rearrange("p g n -> p (g n)").bitcast(FP8X4),
+                scales=scales[:].rearrange("p g n -> p (g n)"),
+                in_=grouped[:].rearrange("p g n -> p (g n)"),
+            )
+            hq[e] = (codes, scales)
+
+        def layer2(e):
+            codes, scales = w2q[e]
+            hcodes, hscales = hq[e]
+            accs = [psum_y.tile([P, C], F32, name=f"acc_y{b}") for b in range(NB)]
+            for h in range(HB):
+                for b in range(NB):
+                    cols = slice(b * P, (b + 1) * P)
+                    nc.tensor.matmul_mx(
+                        out=accs[b][:],
+                        lhsT=codes[:, h, cols].bitcast(FP8X4),
+                        lhsT_scale=scales[:, h, cols],
+                        rhs=hcodes[:, h, :].bitcast(FP8X4),
+                        rhs_scale=hscales[:, h, :],
+                        start=(h == 0),
+                        stop=(h == HB - 1),
+                    )
+            y = hid.tile([P, NB, C], F32, name="y")
+            for b in range(NB):
+                nc.scalar.copy(out=y[:, b, :], in_=accs[b][:])
+                nc.vector.tensor_tensor(
+                    window[b][:].indirect(offsets[:, e * C // 16 : (e + 1) * C // 16]),
+                    y[:, b, :],
+                    gate_sb[:, b, e * C : (e + 1) * C],
+                    MULT,
+                )
+
+        load_w1(0)
+        load_w2(0)
+        nc.sync.dma_start(out=gate_sb[:], in_=gate.rearrange("(b p) s -> p b s", p=P))
+        for e in range(1, E):
+            load_w1(e)
+            layer1(e - 1)
+            layer2(e - 1)
+            load_w2(e)
+        layer1(E - 1)
+        layer2(E - 1)
+        for b in range(NB):
+            nc.sync.dma_start(out=out_v[b], in_=window[b][:])

@@ -20,29 +20,25 @@ PASS = P * PACK
 G = K // PASS
 HB = H // PASS
 NB = N // P
+SPARE = C * PACK // 2
 
 
 def tile_routed_moe_kernel(tc, xT, w1, w2, gate, offs, out):
     nc = tc.nc
-    xT_v = xT.rearrange("(g p j) t -> g p j t", p=P, j=PACK)
+    x_v = xT.rearrange("(g p j) t -> g p j t", p=P, j=PACK)
     w1_v = w1.rearrange("e (g p j) c -> e g p j c", p=P, j=PACK)
-    w2_v = w2.rearrange("e (g p j) c -> e g p j c", p=P, j=PACK)
+    w2_v = w2.rearrange("e (h p j) c -> e h p j c", p=P, j=PACK)
     out_v = out.rearrange("(b p) t -> b p t", p=P)
+    on_vector, on_scalar = nc.vector.tensor_copy, nc.scalar.copy
 
     with ExitStack() as ctx:
         keep = ctx.enter_context(tc.tile_pool(name="keep", bufs=1))
-        raws = ctx.enter_context(tc.tile_pool(name="raws", bufs=6))
-        raws2 = ctx.enter_context(tc.tile_pool(name="raws2", bufs=4))
-        grp = ctx.enter_context(tc.tile_pool(name="grp", bufs=3))
+        staging = ctx.enter_context(tc.tile_pool(name="staging", bufs=7))
+        grp = ctx.enter_context(tc.tile_pool(name="grp", bufs=2))
         cod = ctx.enter_context(tc.tile_pool(name="cod", bufs=8))
         hid = ctx.enter_context(tc.tile_pool(name="hid", bufs=3))
         psum_a = ctx.enter_context(tc.psum_pool(name="psum_a", bufs=4))
-        psum_y = ctx.enter_context(tc.psum_pool(name="psum_y", bufs=2))
-
-        warm_in = keep.tile([P, 1], F32, name="warm_in")
-        warm_out = keep.tile([P, 1], F32, name="warm_out")
-        nc.vector.memset(warm_in[:], 0.0)
-        nc.scalar.activation(warm_out[:], warm_in[:], SILU)
+        psum_y = ctx.enter_context(tc.psum_pool(name="psum_y", bufs=4))
 
         offsets = keep.tile([P, E * C // 16], U16, name="offsets")
         gate_sb = keep.tile([P, NB, E * C], F32, name="gate_sb")
@@ -55,20 +51,32 @@ def tile_routed_moe_kernel(tc, xT, w1, w2, gate, offs, out):
         for g in range(G):
             nc.gpsimd.memset(xs[g][:], 0)
 
+        slots = []
+
+        def load(*sources, at=0):
+            slot = staging.tile([P, PACK * H + SPARE], F32, name="slot", align_bytes=64)
+            views = []
+            slots.append(slot)
+            for src in sources:
+                size = src.shape[1] * src.shape[2]
+                views.append(slot[:, at : at + size].rearrange("p (r c) -> p r c", r=src.shape[1]))
+                nc.sync.dma_start(out=views[-1], in_=src)
+                at += size
+            return views
+
+        def interleave(copy, dst, src):
+            copy(
+                out=dst.rearrange("p (c i j) -> p c j i", i=4, j=PACK),
+                in_=src.rearrange("p j (c i) -> p c j i", i=4),
+            )
+
+        raw_x = [load(x_v[g])[0] for g in range(G)]
+        nc.sync.dma_start(offsets[:], offs)
         for g in range(G):
-            raw = raws.tile([P, PACK, T], F32, name="raw_x", tag="raw")
-            nc.sync.dma_start(out=raw[:], in_=xT_v[g])
-            if g == G - 1:
-                nc.sync.dma_start(offsets[:], offs)
-            for t0, t1, copy in ((0, 512, nc.vector.tensor_copy), (512, 768, nc.scalar.copy)):
+            for t0, t1, copy in ((0, 512, on_scalar), (512, 768, on_scalar)):
                 grouped = grp.tile([P, (t1 - t0) * PACK], BF16, name=f"grp_x{t0}", align_bytes=64)
-                copy(
-                    out=grouped[:].rearrange("p (c i j) -> p c j i", i=4, j=PACK),
-                    in_=raw[:, :, t0:t1].rearrange("p j (c i) -> p c j i", i=4),
-                )
-                nc.vector.quantize_mx(
-                    out=xw[g][:, t0:t1].bitcast(FP8X4), scales=xs[g][:, t0:t1], in_=grouped[:]
-                )
+                interleave(copy, grouped[:], raw_x[g][:, :, t0:t1])
+                nc.vector.quantize_mx(out=xw[g][:, t0:t1].bitcast(FP8X4), scales=xs[g][:, t0:t1], in_=grouped[:])
         half = E * C // 2
         for s in range(2):
             for g in range(G):
@@ -78,51 +86,46 @@ def tile_routed_moe_kernel(tc, xT, w1, w2, gate, offs, out):
 
         w1q = {}
         w2q = {}
-
-        def load_w1(e):
-            for g in range(G):
-                raw = raws.tile([P, PACK, H], F32, name="raw_w1", tag="raw")
-                last = e == E - 1 and g == G - 1
-                for c0 in range(0, H, PASS if last else H):
-                    c1 = c0 + (PASS if last else H)
-                    nc.sync.dma_start(out=raw[:, :, c0:c1], in_=w1_v[e, g][:, :, c0:c1])
-                for h in range(HB):
-                    grouped = grp.tile([P, PASS * PACK], BF16, name=f"grp_w1_{h}", align_bytes=64)
-                    dst = grouped[:].rearrange("p (t m j) -> p m j t", t=PACK, j=PACK)
-                    src = raw[:, :, h * PASS : (h + 1) * PASS].rearrange("p j (m t) -> p m j t", t=PACK)
-                    cut = 48 if last else (P if h == 0 else 0)
-                    if cut > 0:
-                        nc.scalar.copy(out=dst[:, :cut], in_=src[:, :cut])
-                    if cut < P:
-                        nc.vector.tensor_copy(out=dst[:, cut:], in_=src[:, cut:])
-                    codes = cod.tile([P, PASS], U32, name="w1_codes", align_bytes=64)
-                    scales = cod.tile([P, PASS], U8, name="w1_scales", align_bytes=64)
-                    nc.vector.quantize_mx(out=codes[:].bitcast(FP8X4), scales=scales[:], in_=grouped[:])
-                    w1q[e, g, h] = (codes, scales)
-
-        def load_w2(e):
-            codes = hid.tile([P, HB, N], U32, name="w2_codes", align_bytes=64)
-            scales = hid.tile([P, HB, N], U8, name="w2_scales", align_bytes=64)
-            for h in range(HB):
-                raw = raws2.tile([P, PACK, N], F32, name="raw_w2")
-                nc.sync.dma_start(out=raw[:], in_=w2_v[e, h])
-                grouped = grp.tile([P, N * PACK], BF16, name="grp_w2", align_bytes=64)
-                dst = grouped[:].rearrange("p (c i j) -> p c j i", i=4, j=PACK)
-                src = raw[:].rearrange("p j (c i) -> p c j i", i=4)
-                cut = 24 if e == E - 1 and h == HB - 1 else N // 4
-                if cut > 0:
-                    nc.scalar.copy(out=dst[:, :cut], in_=src[:, :cut])
-                if cut < N // 4:
-                    nc.vector.tensor_copy(out=dst[:, cut:], in_=src[:, cut:])
-                nc.vector.quantize_mx(out=codes[:, h, :].bitcast(FP8X4), scales=scales[:, h, :], in_=grouped[:])
-            w2q[e] = (codes, scales)
-
         hq = {}
 
-        def layer1(e):
-            slots = slice(e * C, (e + 1) * C)
-            grouped = hid.tile([P, HB, C * PACK], BF16, name="grp_h", align_bytes=64)
-            for h in range(HB):
+        def quantize_w2(e, h, b0, rows, copy):
+            width = rows.shape[2]
+            grouped = grp.tile([P, width * PACK], BF16, name="grp_w2", bufs=4, align_bytes=64)
+            interleave(copy, grouped[:], rows)
+            codes = hid.tile([P, width], U32, name="w2_codes", bufs=8, align_bytes=64)
+            scales = hid.tile([P, width], U8, name="w2_scales", bufs=8, align_bytes=64)
+            nc.vector.quantize_mx(out=codes[:].bitcast(FP8X4), scales=scales[:], in_=grouped[:])
+            for b in range(width // P):
+                w2q[e, h, b0 + b] = (codes[:, b * P : (b + 1) * P], scales[:, b * P : (b + 1) * P])
+            return grouped
+
+        def quantize_w1(e, g, h, shares, parts=1):
+            grouped = grp.tile([P, PASS * PACK], BF16, name=f"grp_w1_{h}", bufs=3, align_bytes=64)
+            dst = grouped[:].rearrange("p (t m j) -> p m j t", t=PACK, j=PACK)
+            for rows, m0, copy in shares:
+                src = rows.rearrange("p j (m t) -> p m j t", t=PACK)
+                copy(out=dst[:, m0 : m0 + src.shape[1]], in_=src)
+            codes = cod.tile([P, PASS], U32, name="w1_codes", align_bytes=64)
+            scales = cod.tile([P, PASS], U8, name="w1_scales", align_bytes=64)
+            width = PASS // parts
+            for c0 in range(0, PASS, width):
+                cols = slice(c0, c0 + width)
+                nc.vector.quantize_mx(
+                    out=codes[:, cols].bitcast(FP8X4),
+                    scales=scales[:, cols],
+                    in_=grouped[:, c0 * PACK : (c0 + width) * PACK],
+                )
+            w1q[e, g, h] = (codes, scales)
+            return grouped
+
+        def prepare_w1(e, g, rows):
+            spent = quantize_w1(e, g, 1, [(rows[:, :, PASS:], 0, on_vector)])
+            quantize_w1(e, g, 0, [(rows[:, :, :PASS], 0, on_scalar)])
+            return spent
+
+        def layer1(e, hs, grouped):
+            tokens = slice(e * C, (e + 1) * C)
+            for i, h in enumerate(hs):
                 acc = psum_a.tile([P, PACK, C], F32, name="acc_a")
                 for t in range(PACK):
                     for g in range(G):
@@ -131,60 +134,93 @@ def tile_routed_moe_kernel(tc, xT, w1, w2, gate, offs, out):
                             out=acc[:, t, :],
                             lhsT=codes[:, t * P : (t + 1) * P].bitcast(FP8X4),
                             lhsT_scale=scales[:, t * P : (t + 1) * P],
-                            rhs=gw[:, g, slots].bitcast(FP8X4),
-                            rhs_scale=gs[:, g, slots],
+                            rhs=gw[:, g, tokens].bitcast(FP8X4),
+                            rhs_scale=gs[:, g, tokens],
                             start=(g == 0),
                             stop=(g == G - 1),
                         )
                 nc.scalar.activation(
-                    grouped[:, h, :].rearrange("p (n t) -> p n t", t=PACK),
+                    grouped[:, i * C * PACK : (i + 1) * C * PACK].rearrange("p (n t) -> p n t", t=PACK),
                     acc[:].rearrange("p t n -> p n t"),
                     SILU,
                 )
-            codes = hid.tile([P, HB, C], U32, name="h_codes", align_bytes=64)
-            scales = hid.tile([P, HB, C], U8, name="h_scales", align_bytes=64)
-            nc.vector.quantize_mx(
-                out=codes[:].rearrange("p g n -> p (g n)").bitcast(FP8X4),
-                scales=scales[:].rearrange("p g n -> p (g n)"),
-                in_=grouped[:].rearrange("p g n -> p (g n)"),
-            )
-            hq[e] = (codes, scales)
 
-        def layer2(e):
-            codes, scales = w2q[e]
-            hcodes, hscales = hq[e]
-            accs = [psum_y.tile([P, C], F32, name=f"acc_y{b}") for b in range(NB)]
-            for h in range(HB):
-                for b in range(NB):
-                    cols = slice(b * P, (b + 1) * P)
+        def quantize_h(e, hs, grouped):
+            codes = hid.tile([P, len(hs) * C], U32, name="h_codes", align_bytes=64)
+            scales = hid.tile([P, len(hs) * C], U8, name="h_scales", align_bytes=64)
+            nc.vector.quantize_mx(out=codes[:].bitcast(FP8X4), scales=scales[:], in_=grouped)
+            for i, h in enumerate(hs):
+                hq[e, h] = (codes[:, i * C : (i + 1) * C], scales[:, i * C : (i + 1) * C])
+
+        def layer2(e, bs, room):
+            acc = psum_y.tile([P, len(bs), C], F32, name="acc_y")
+            for i, b in enumerate(bs):
+                for h in range(HB):
                     nc.tensor.matmul_mx(
-                        out=accs[b][:],
-                        lhsT=codes[:, h, cols].bitcast(FP8X4),
-                        lhsT_scale=scales[:, h, cols],
-                        rhs=hcodes[:, h, :].bitcast(FP8X4),
-                        rhs_scale=hscales[:, h, :],
+                        out=acc[:, i, :],
+                        lhsT=w2q[e, h, b][0].bitcast(FP8X4),
+                        lhsT_scale=w2q[e, h, b][1],
+                        rhs=hq[e, h][0].bitcast(FP8X4),
+                        rhs_scale=hq[e, h][1],
                         start=(h == 0),
                         stop=(h == HB - 1),
                     )
-            y = hid.tile([P, NB, C], F32, name="y")
-            for b in range(NB):
-                nc.scalar.copy(out=y[:, b, :], in_=accs[b][:])
+            y = room[:, : 2 * len(bs) * C].bitcast(F32).rearrange("p (b n) -> p b n", n=C)
+            nc.scalar.copy(out=y, in_=acc[:])
+            for i, b in enumerate(bs):
                 nc.vector.tensor_tensor(
                     window[b][:].indirect(offsets[:, e * C // 16 : (e + 1) * C // 16]),
-                    y[:, b, :],
+                    y[:, i, :],
                     gate_sb[:, b, e * C : (e + 1) * C],
                     MULT,
                 )
 
-        load_w1(0)
-        load_w2(0)
-        nc.sync.dma_start(out=gate_sb[:], in_=gate.rearrange("(b p) s -> p b s", p=P))
-        for e in range(1, E):
-            load_w1(e)
-            layer1(e - 1)
-            layer2(e - 1)
-            load_w2(e)
-        layer1(E - 1)
-        layer2(E - 1)
+        last = E - 1
+        for e in range(last):
+            raw_w1 = [load(w1_v[e, g])[0] for g in range(G)]
+            raw_w2 = load(w2[e].rearrange("(h p j) c -> p h (j c)", p=P, j=PACK))[0]
+            if e == 0:
+                nc.sync.dma_start(out=gate_sb[:], in_=gate.rearrange("(b p) s -> p b s", p=P))
+            spent = prepare_w1(e, 0, raw_w1[0])
+            if e == last - 1:
+                layer2(e - 1, range(NB), spent)
+            spent = prepare_w1(e, 1, raw_w1[1])
+            if 0 < e < last - 1:
+                layer2(e - 1, range(NB), spent)
+            if e < last - 1:
+                grouped_h = hid.tile([P, HB * C * PACK], BF16, name="grp_h", align_bytes=64)
+                layer1(e, range(HB), grouped_h[:])
+                quantize_h(e, range(HB), grouped_h[:])
+            for h in range(HB):
+                quantize_w2(e, h, 0, raw_w2[:, h, :].rearrange("p (j c) -> p j c", j=PACK), on_scalar)
+
+        first = load(w1_v[last, 0][:, :, :PASS], w1_v[last, 1][:, :, :PASS], at=SPARE)
+        second = load(w1_v[last, 0][:, :, PASS:], w1_v[last, 1][:, :, PASS : PASS + 256], w1_v[last, 1][:, :, PASS + 256 :])
+        raw_w2 = load(*[w2_v[last, h] for h in range(HB)])
+        shares = {}
+        for key, rows in (((0, 0), first[0]), ((0, 1), first[1]), ((1, 0), second[0])):
+            shares[key] = [(rows[:, :, :256], 0, on_scalar), (rows[:, :, 256:], 64, on_vector)]
+        shares[0, 0] = [(first[0], 0, on_vector)]
+        shares[1, 0] = [(second[0][:, :, :192], 0, on_scalar), (second[0][:, :, 192:], 48, on_vector)]
+        shares[1, 1] = [(second[1], 0, on_scalar), (second[2], 64, on_vector)]
+
+        first_slot = slots[-3]
+        quantize_w1(last, 0, 0, shares[0, 0])
+        grouped_h = first_slot[:, : 2 * SPARE].bitcast(BF16)
+        layer1(last - 1, (1, 0), grouped_h)
+        quantize_h(last - 1, (1, 0), grouped_h)
+        quantize_w1(last, 1, 0, shares[0, 1])
+        quantize_w1(last, 0, 1, shares[1, 0])
+        spent = quantize_w1(last, 1, 1, shares[1, 1], parts=PACK)
+        last_h = hid.tile([P, C * PACK], BF16, name="grp_h", align_bytes=64)
+        halves = (second[1][:, 0, :].bitcast(BF16), last_h[:])
+        for h in range(HB):
+            layer1(last, [h], halves[h])
+        quantize_h(last, [0], halves[0])
+        rooms = [quantize_w2(last, h, 0, raw_w2[h], copy) for h, copy in enumerate((on_scalar, on_vector))]
+        quantize_h(last, [1], halves[1])
+        layer2(last - 1, [0], spent)
+        layer2(last - 1, [1], rooms[0])
         for b in range(NB):
+            layer2(last, [b], rooms[1][:, 2 * b * C :])
             nc.sync.dma_start(out=out_v[b], in_=window[b][:])

@@ -28,6 +28,7 @@ def tile_routed_moe_kernel(tc, xT, w1, w2, gate, offs, out):
     x_v = xT.rearrange("(g p j) t -> g p j t", p=P, j=PACK)
     w1_v = w1.rearrange("e (g p j) c -> e g p j c", p=P, j=PACK)
     w2_v = w2.rearrange("e (h p j) c -> e h p j c", p=P, j=PACK)
+    gate_v = gate.rearrange("(b p) s -> p b s", p=P)
     out_v = out.rearrange("(b p) t -> b p t", p=P)
     on_vector, on_scalar = nc.vector.tensor_copy, nc.scalar.copy
 
@@ -41,7 +42,7 @@ def tile_routed_moe_kernel(tc, xT, w1, w2, gate, offs, out):
         psum_y = ctx.enter_context(tc.psum_pool(name="psum_y", bufs=4))
 
         offsets = keep.tile([P, E * C // 16], U16, name="offsets")
-        gate_sb = keep.tile([P, NB, E * C], F32, name="gate_sb")
+        gate_sb = keep.tile([P, NB, (E - 1) * C], F32, name="gate_sb")
         xw = [keep.tile([P, T], U32, name=f"xw{g}", align_bytes=64) for g in range(G)]
         xs = [keep.tile([P, T], U8, name=f"xs{g}", align_bytes=64) for g in range(G)]
         gw = keep.tile([P, G, E * C], U32, name="gw", align_bytes=64)
@@ -171,7 +172,7 @@ def tile_routed_moe_kernel(tc, xT, w1, w2, gate, offs, out):
                 nc.vector.tensor_tensor(
                     window[b][:].indirect(offsets[:, e * C // 16 : (e + 1) * C // 16]),
                     y[:, i, :],
-                    gate_sb[:, b, e * C : (e + 1) * C],
+                    gate_last[:, b, :] if e == last else gate_sb[:, b, e * C : (e + 1) * C],
                     MULT,
                 )
 
@@ -180,7 +181,7 @@ def tile_routed_moe_kernel(tc, xT, w1, w2, gate, offs, out):
             raw_w1 = [load(w1_v[e, g])[0] for g in range(G)]
             raw_w2 = load(w2[e].rearrange("(h p j) c -> p h (j c)", p=P, j=PACK))[0]
             if e == 0:
-                nc.sync.dma_start(out=gate_sb[:], in_=gate.rearrange("(b p) s -> p b s", p=P))
+                nc.sync.dma_start(out=gate_sb[:], in_=gate_v[:, :, : last * C])
             spent = prepare_w1(e, 0, raw_w1[0])
             if e == last - 1:
                 layer2(e - 1, range(NB), spent)
@@ -191,18 +192,18 @@ def tile_routed_moe_kernel(tc, xT, w1, w2, gate, offs, out):
                 grouped_h = hid.tile([P, HB * C * PACK], BF16, name="grp_h", align_bytes=64)
                 layer1(e, range(HB), grouped_h[:])
                 quantize_h(e, range(HB), grouped_h[:])
-            for h in range(HB):
-                quantize_w2(e, h, 0, raw_w2[:, h, :].rearrange("p (j c) -> p j c", j=PACK), on_scalar)
+            for h, copy in enumerate((on_scalar, on_vector)):
+                quantize_w2(e, h, 0, raw_w2[:, h, :].rearrange("p (j c) -> p j c", j=PACK), copy)
 
         first = load(w1_v[last, 0][:, :, :PASS], w1_v[last, 1][:, :, :PASS], at=SPARE)
         second = load(w1_v[last, 0][:, :, PASS:], w1_v[last, 1][:, :, PASS : PASS + 256], w1_v[last, 1][:, :, PASS + 256 :])
-        raw_w2 = load(*[w2_v[last, h] for h in range(HB)])
+        *raw_w2, gate_last = load(*[w2_v[last, h] for h in range(HB)], gate_v[:, :, last * C :])
         shares = {}
         for key, rows in (((0, 0), first[0]), ((0, 1), first[1]), ((1, 0), second[0])):
             shares[key] = [(rows[:, :, :256], 0, on_scalar), (rows[:, :, 256:], 64, on_vector)]
         shares[0, 0] = [(first[0], 0, on_vector)]
         shares[1, 0] = [(second[0][:, :, :192], 0, on_scalar), (second[0][:, :, 192:], 48, on_vector)]
-        shares[1, 1] = [(second[1], 0, on_scalar), (second[2], 64, on_vector)]
+        shares[1, 1] = [(second[1], 0, on_scalar), (second[2][:, :, :64], 64, on_scalar), (second[2][:, :, 64:], 80, on_vector)]
 
         first_slot = slots[-3]
         quantize_w1(last, 0, 0, shares[0, 0])

@@ -201,8 +201,6 @@ def tile_routed_moe_kernel(tc, xT, w1, w2, gate, offs, out):
         shares = {}
         for key, rows in (((0, 0), first[0]), ((0, 1), first[1]), ((1, 0), second[0])):
             shares[key] = [(rows[:, :, :256], 0, on_scalar), (rows[:, :, 256:], 64, on_vector)]
-        shares[0, 0] = [(first[0], 0, on_vector)]
-        shares[1, 0] = [(second[0][:, :, :192], 0, on_scalar), (second[0][:, :, 192:], 48, on_vector)]
         shares[1, 1] = [(second[1], 0, on_scalar), (second[2][:, :, :64], 64, on_scalar), (second[2][:, :, 64:], 80, on_vector)]
 
         first_slot = slots[-3]
@@ -211,8 +209,9 @@ def tile_routed_moe_kernel(tc, xT, w1, w2, gate, offs, out):
         layer1(last - 1, (1, 0), grouped_h)
         quantize_h(last - 1, (1, 0), grouped_h)
         quantize_w1(last, 1, 0, shares[0, 1])
+        layer2(last - 1, [0], first[1][:, 0, :C].bitcast(BF16))
         quantize_w1(last, 0, 1, shares[1, 0])
-        spent = quantize_w1(last, 1, 1, shares[1, 1], parts=PACK)
+        quantize_w1(last, 1, 1, shares[1, 1], parts=PACK)
         last_h = hid.tile([P, C * PACK], BF16, name="grp_h", align_bytes=64)
         halves = (second[1][:, 0, :].bitcast(BF16), last_h[:])
         for h in range(HB):
@@ -220,7 +219,6 @@ def tile_routed_moe_kernel(tc, xT, w1, w2, gate, offs, out):
         quantize_h(last, [0], halves[0])
         rooms = [quantize_w2(last, h, 0, raw_w2[h], copy) for h, copy in enumerate((on_scalar, on_vector))]
         quantize_h(last, [1], halves[1])
-        layer2(last - 1, [0], spent)
         layer2(last - 1, [1], rooms[0])
         for b in range(NB):
             layer2(last, [b], rooms[1][:, 2 * b * C :])

@@ -20,7 +20,6 @@ PASS = P * PACK
 G = K // PASS
 HB = H // PASS
 NB = N // P
-SPARE = C * PACK // 2
 
 
 def tile_routed_moe_kernel(tc, xT, w1, w2, gate, offs, out):
@@ -45,19 +44,15 @@ def tile_routed_moe_kernel(tc, xT, w1, w2, gate, offs, out):
         gate_sb = keep.tile([P, NB, (E - 1) * C], F32, name="gate_sb")
         xw = [keep.tile([P, T], U32, name=f"xw{g}", align_bytes=64) for g in range(G)]
         xs = [keep.tile([P, T], U8, name=f"xs{g}", align_bytes=64) for g in range(G)]
-        gw = keep.tile([P, G, E * C], U32, name="gw", align_bytes=64)
-        gs = keep.tile([P, G, E * C], U8, name="gs", align_bytes=64)
         window = [keep.tile([P, T], F32, name=f"window{b}") for b in range(NB)]
 
         for g in range(G):
             nc.gpsimd.memset(xs[g][:], 0)
 
-        slots = []
-
-        def load(*sources, at=0):
-            slot = staging.tile([P, PACK * H + SPARE], F32, name="slot", align_bytes=64)
+        def load(*sources):
+            slot = staging.tile([P, PACK * H], F32, name="slot", align_bytes=64)
             views = []
-            slots.append(slot)
+            at = 0
             for src in sources:
                 size = src.shape[1] * src.shape[2]
                 views.append(slot[:, at : at + size].rearrange("p (r c) -> p r c", r=src.shape[1]))
@@ -73,39 +68,63 @@ def tile_routed_moe_kernel(tc, xT, w1, w2, gate, offs, out):
 
         raw_x = [load(x_v[g])[0] for g in range(G)]
         nc.sync.dma_start(offsets[:], offs)
+        x_deal = (((0, 512, on_vector), (512, 768, on_scalar)), ((0, 512, on_scalar), (512, 768, on_vector)))
         for g in range(G):
-            for t0, t1, copy in ((0, 512, on_scalar), (512, 768, on_scalar)):
+            for t0, t1, copy in x_deal[g]:
                 grouped = grp.tile([P, (t1 - t0) * PACK], BF16, name=f"grp_x{t0}", align_bytes=64)
                 interleave(copy, grouped[:], raw_x[g][:, :, t0:t1])
                 nc.vector.quantize_mx(out=xw[g][:, t0:t1].bitcast(FP8X4), scales=xs[g][:, t0:t1], in_=grouped[:])
-        half = E * C // 2
-        for s in range(2):
+
+        xq = {}
+
+        def gather(e0):
+            gw = grp.tile([P, G, 2 * C], U32, name="gw", align_bytes=64)
+            gs = grp.tile([P, G, 2 * C], U8, name="gs", align_bytes=64)
+            sl = offsets[:, e0 * C // 16 : (e0 + 2) * C // 16]
             for g in range(G):
-                sl = offsets[:, s * half // 16 : (s + 1) * half // 16]
-                nc.vector.tensor_copy(out=gw[:, g, s * half : (s + 1) * half], in_=xw[g][:].indirect(sl))
-                nc.vector.tensor_copy(out=gs[:, g, s * half : (s + 1) * half], in_=xs[g][:].indirect(sl))
+                nc.vector.tensor_copy(out=gw[:, g, :], in_=xw[g][:].indirect(sl))
+                nc.vector.tensor_copy(out=gs[:, g, :], in_=xs[g][:].indirect(sl))
+                for i in range(2):
+                    xq[e0 + i, g] = (gw[:, g, i * C : (i + 1) * C], gs[:, g, i * C : (i + 1) * C])
+
+        gather(0)
+        gather(2)
 
         w1q = {}
         w2q = {}
         hq = {}
 
-        def quantize_w2(e, h, b0, rows, copy):
-            width = rows.shape[2]
-            grouped = grp.tile([P, width * PACK], BF16, name="grp_w2", bufs=4, align_bytes=64)
-            interleave(copy, grouped[:], rows)
-            codes = hid.tile([P, width], U32, name="w2_codes", bufs=8, align_bytes=64)
-            scales = hid.tile([P, width], U8, name="w2_scales", bufs=8, align_bytes=64)
-            nc.vector.quantize_mx(out=codes[:].bitcast(FP8X4), scales=scales[:], in_=grouped[:])
-            for b in range(width // P):
-                w2q[e, h, b0 + b] = (codes[:, b * P : (b + 1) * P], scales[:, b * P : (b + 1) * P])
+        def quantize_w2(e, h, rows, shares, parts=1):
+            grouped = grp.tile([P, N * PACK], BF16, name="grp_w2", bufs=4, align_bytes=64)
+            for c0, c1, copy in shares:
+                interleave(copy, grouped[:, c0 * PACK : c1 * PACK], rows[:, :, c0:c1])
+            codes = hid.tile([P, N], U32, name="w2_codes", bufs=8, align_bytes=64)
+            scales = hid.tile([P, N], U8, name="w2_scales", bufs=8, align_bytes=64)
+            width = N // parts
+            for c0 in range(0, N, width):
+                cols = slice(c0, c0 + width)
+                nc.vector.quantize_mx(
+                    out=codes[:, cols].bitcast(FP8X4),
+                    scales=scales[:, cols],
+                    in_=grouped[:, c0 * PACK : (c0 + width) * PACK],
+                )
+            for b in range(NB):
+                w2q[e, h, b] = (codes[:, b * P : (b + 1) * P], scales[:, b * P : (b + 1) * P])
             return grouped
 
-        def quantize_w1(e, g, h, shares, parts=1):
-            grouped = grp.tile([P, PASS * PACK], BF16, name=f"grp_w1_{h}", bufs=3, align_bytes=64)
+        def copy_w1(h, shares, grouped=None):
+            if grouped is None:
+                grouped = grp.tile([P, PASS * PACK], BF16, name=f"grp_w1_{h}", bufs=3, align_bytes=64)
             dst = grouped[:].rearrange("p (t m j) -> p m j t", t=PACK, j=PACK)
-            for rows, m0, copy in shares:
+            for rows, m0, t0, t1, copy in shares:
                 src = rows.rearrange("p j (m t) -> p m j t", t=PACK)
-                copy(out=dst[:, m0 : m0 + src.shape[1]], in_=src)
+                copy(out=dst[:, m0 : m0 + src.shape[1], :, t0:t1], in_=src[:, :, :, t0:t1])
+            return grouped
+
+        def by_pairs(rows, m0=0):
+            return [(rows, m0, 0, 2, on_vector), (rows, m0, 2, 4, on_scalar)]
+
+        def quantize_w1(e, g, h, grouped, parts=1):
             codes = cod.tile([P, PASS], U32, name="w1_codes", align_bytes=64)
             scales = cod.tile([P, PASS], U8, name="w1_scales", align_bytes=64)
             width = PASS // parts
@@ -119,36 +138,42 @@ def tile_routed_moe_kernel(tc, xT, w1, w2, gate, offs, out):
             w1q[e, g, h] = (codes, scales)
             return grouped
 
-        def prepare_w1(e, g, rows):
-            spent = quantize_w1(e, g, 1, [(rows[:, :, PASS:], 0, on_vector)])
-            quantize_w1(e, g, 0, [(rows[:, :, :PASS], 0, on_scalar)])
-            return spent
+        def by_columns(rows, m1):
+            shares = [(rows[:, :, : m1 * PACK], 0, 0, PACK, on_vector), (rows[:, :, m1 * PACK :], m1, 0, PACK, on_scalar)]
+            return [share for share in shares if share[0].shape[2]]
 
-        def layer1(e, hs, grouped):
-            tokens = slice(e * C, (e + 1) * C)
-            for i, h in enumerate(hs):
-                acc = psum_a.tile([P, PACK, C], F32, name="acc_a")
-                for t in range(PACK):
-                    for g in range(G):
-                        codes, scales = w1q[e, g, h]
-                        nc.tensor.matmul_mx(
-                            out=acc[:, t, :],
-                            lhsT=codes[:, t * P : (t + 1) * P].bitcast(FP8X4),
-                            lhsT_scale=scales[:, t * P : (t + 1) * P],
-                            rhs=gw[:, g, tokens].bitcast(FP8X4),
-                            rhs_scale=gs[:, g, tokens],
-                            start=(g == 0),
-                            stop=(g == G - 1),
-                        )
-                nc.scalar.activation(
-                    grouped[:, i * C * PACK : (i + 1) * C * PACK].rearrange("p (n t) -> p n t", t=PACK),
-                    acc[:].rearrange("p t n -> p n t"),
-                    SILU,
+        def prepare_half(e, g, h, shares):
+            return quantize_w1(e, g, h, copy_w1(h, shares))
+
+        def spent(rows):
+            return rows[:, :1, :C]
+
+        def layer1(e, h, grouped, one_group=False):
+            acc = psum_a.tile([P, PACK, C], F32, name="acc_a")
+            if one_group:
+                passes = [(t, g, (g, t) == (0, 0), (g, t) == (G - 1, PACK - 1)) for g in range(G) for t in range(PACK)]
+            else:
+                passes = [(t, g, g == 0, g == G - 1) for t in range(PACK) for g in range(G)]
+            for t, g, start, stop in passes:
+                codes, scales = w1q[e, g, h]
+                nc.tensor.matmul_mx(
+                    out=acc[:, t, :],
+                    lhsT=codes[:, t * P : (t + 1) * P].bitcast(FP8X4),
+                    lhsT_scale=scales[:, t * P : (t + 1) * P],
+                    rhs=xq[e, g][0].bitcast(FP8X4),
+                    rhs_scale=xq[e, g][1],
+                    start=start,
+                    stop=stop,
                 )
+            nc.scalar.activation(
+                grouped.rearrange("p (n t) -> p n t", t=PACK),
+                acc[:].rearrange("p t n -> p n t"),
+                SILU,
+            )
 
         def quantize_h(e, hs, grouped):
-            codes = hid.tile([P, len(hs) * C], U32, name="h_codes", align_bytes=64)
-            scales = hid.tile([P, len(hs) * C], U8, name="h_scales", align_bytes=64)
+            codes = hid.tile([P, len(hs) * C], U32, name="h_codes", bufs=5, align_bytes=64)
+            scales = hid.tile([P, len(hs) * C], U8, name="h_scales", bufs=5, align_bytes=64)
             nc.vector.quantize_mx(out=codes[:].bitcast(FP8X4), scales=scales[:], in_=grouped)
             for i, h in enumerate(hs):
                 hq[e, h] = (codes[:, i * C : (i + 1) * C], scales[:, i * C : (i + 1) * C])
@@ -166,60 +191,84 @@ def tile_routed_moe_kernel(tc, xT, w1, w2, gate, offs, out):
                         start=(h == 0),
                         stop=(h == HB - 1),
                     )
-            y = room[:, : 2 * len(bs) * C].bitcast(F32).rearrange("p (b n) -> p b n", n=C)
-            nc.scalar.copy(out=y, in_=acc[:])
-            for i, b in enumerate(bs):
-                nc.vector.tensor_tensor(
-                    window[b][:].indirect(offsets[:, e * C // 16 : (e + 1) * C // 16]),
-                    y[:, i, :],
-                    gate_last[:, b, :] if e == last else gate_sb[:, b, e * C : (e + 1) * C],
-                    MULT,
-                )
+            nc.scalar.copy(out=room, in_=acc[:])
+
+        def scatter(e, b, y):
+            nc.vector.tensor_tensor(
+                window[b][:].indirect(offsets[:, e * C // 16 : (e + 1) * C // 16]),
+                y,
+                gate_last[:, b, :] if e == last else gate_sb[:, b, e * C : (e + 1) * C],
+                MULT,
+            )
+
+        def finish(e, b, room):
+            layer2(e, [b], room)
+            scatter(e, b, room[:, 0, :])
+
+        def load_w2(e):
+            raw = load(w2[e].rearrange("(h p j) c -> p h (j c)", p=P, j=PACK))[0]
+            return [raw[:, h, :].rearrange("p (j c) -> p j c", j=PACK) for h in range(HB)]
+
+        def prepare_w2(e, raw):
+            for h, copy in enumerate((on_scalar, on_vector)):
+                quantize_w2(e, h, raw[h], [(0, N, copy)])
 
         last = E - 1
+        half = C * PACK
         for e in range(last):
             raw_w1 = [load(w1_v[e, g])[0] for g in range(G)]
-            raw_w2 = load(w2[e].rearrange("(h p j) c -> p h (j c)", p=P, j=PACK))[0]
+            raw_w2 = load_w2(e)
             if e == 0:
                 nc.sync.dma_start(out=gate_sb[:], in_=gate_v[:, :, : last * C])
-            spent = prepare_w1(e, 0, raw_w1[0])
-            if e == last - 1:
-                layer2(e - 1, range(NB), spent)
-            spent = prepare_w1(e, 1, raw_w1[1])
-            if 0 < e < last - 1:
-                layer2(e - 1, range(NB), spent)
-            if e < last - 1:
-                grouped_h = hid.tile([P, HB * C * PACK], BF16, name="grp_h", align_bytes=64)
-                layer1(e, range(HB), grouped_h[:])
-                quantize_h(e, range(HB), grouped_h[:])
-            for h, copy in enumerate((on_scalar, on_vector)):
-                quantize_w2(e, h, 0, raw_w2[:, h, :].rearrange("p (j c) -> p j c", j=PACK), copy)
+            for g, shares in enumerate(((0, 96), (64, 64) if e < last - 1 else (80, 80))):
+                for h in range(HB):
+                    prepare_half(e, g, h, by_columns(raw_w1[g][:, :, h * PASS : (h + 1) * PASS], shares[h]))
+            grouped_h = hid.tile([P, HB * half], BF16, name="grp_h", align_bytes=64)
+            for h in range(HB):
+                layer1(e, h, grouped_h[:, h * half : (h + 1) * half], one_group=True)
+            prepare_w2(e, raw_w2)
+            for hs in ([range(HB)] if e < last - 1 else [[0], [1]]):
+                quantize_h(e, hs, grouped_h[:, hs[0] * half : (hs[-1] + 1) * half])
+            y = hid.tile([P, NB, C], F32, name="y")
+            for b in range(NB if e < last - 1 else 1):
+                finish(e, b, y[:, b : b + 1, :])
+            if e == 1:
+                gather(4)
 
-        first = load(w1_v[last, 0][:, :, :PASS], w1_v[last, 1][:, :, :PASS], at=SPARE)
-        second = load(w1_v[last, 0][:, :, PASS:], w1_v[last, 1][:, :, PASS : PASS + 256], w1_v[last, 1][:, :, PASS + 256 :])
+        first = load(w1_v[last, 0])[0]
+        second = load(w1_v[last, 1][:, :, :PASS], w1_v[last, 1][:, :, PASS:])
         *raw_w2, gate_last = load(*[w2_v[last, h] for h in range(HB)], gate_v[:, :, last * C :])
-        shares = {}
-        for key, rows in (((0, 0), first[0]), ((0, 1), first[1]), ((1, 0), second[0])):
-            shares[key] = [(rows[:, :, :256], 0, on_scalar), (rows[:, :, 256:], 64, on_vector)]
-        shares[1, 1] = [(second[1], 0, on_scalar), (second[2][:, :, :64], 64, on_scalar), (second[2][:, :, 64:], 80, on_vector)]
-
-        first_slot = slots[-3]
-        quantize_w1(last, 0, 0, shares[0, 0])
-        grouped_h = first_slot[:, : 2 * SPARE].bitcast(BF16)
-        layer1(last - 1, (1, 0), grouped_h)
-        quantize_h(last - 1, (1, 0), grouped_h)
-        quantize_w1(last, 1, 0, shares[0, 1])
-        layer2(last - 1, [0], first[1][:, 0, :C].bitcast(BF16))
-        quantize_w1(last, 0, 1, shares[1, 0])
-        quantize_w1(last, 1, 1, shares[1, 1], parts=PACK)
-        last_h = hid.tile([P, C * PACK], BF16, name="grp_h", align_bytes=64)
-        halves = (second[1][:, 0, :].bitcast(BF16), last_h[:])
+        prepare_half(last, 0, 0, by_columns(first[:, :, :PASS], 32))
+        prepare_half(last, 0, 1, by_columns(first[:, :, PASS:], 80))
+        prepare_half(last, 1, 0, by_columns(second[0], 80))
+        grouped = copy_w1(1, by_columns(second[1], 84))
+        quantize_w1(last, 1, 1, grouped, parts=PACK)
+        last_h = hid.tile([P, half], BF16, name="grp_h", align_bytes=64)
+        halves = (second[1][:, 0, PASS - half // 2 :].bitcast(BF16), last_h[:])
         for h in range(HB):
-            layer1(last, [h], halves[h])
+            layer1(last, h, halves[h], one_group=True)
         quantize_h(last, [0], halves[0])
-        rooms = [quantize_w2(last, h, 0, raw_w2[h], copy) for h, copy in enumerate((on_scalar, on_vector))]
+        grouped = [grp.tile([P, HB, P * PACK], BF16, name="grp_w2", bufs=4, align_bytes=64) for b in range(NB)]
+        for h in range(HB):
+            for b in range(NB):
+                copy = on_scalar if (h, b) == (0, 1) else on_vector
+                interleave(copy, grouped[b][:, h, :], raw_w2[h][:, :, b * P : (b + 1) * P])
+
+        def quantize_block(b):
+            codes = hid.tile([P, HB, P], U32, name="w2_codes", bufs=8, align_bytes=64)
+            scales = hid.tile([P, HB, P], U8, name="w2_scales", bufs=8, align_bytes=64)
+            nc.vector.quantize_mx(
+                out=codes[:].rearrange("p h c -> p (h c)").bitcast(FP8X4),
+                scales=scales[:].rearrange("p h c -> p (h c)"),
+                in_=grouped[b][:].rearrange("p h c -> p (h c)"),
+            )
+            for h in range(HB):
+                w2q[last, h, b] = (codes[:, h, :], scales[:, h, :])
+
+        quantize_block(0)
         quantize_h(last, [1], halves[1])
-        layer2(last - 1, [1], rooms[0])
+        quantize_block(1)
+        finish(last - 1, 1, raw_w2[1][:, :1, P:])
         for b in range(NB):
-            layer2(last, [b], rooms[1][:, 2 * b * C :])
+            finish(last, b, raw_w2[0][:, b : b + 1, :P])
             nc.sync.dma_start(out=out_v[b], in_=window[b][:])

@@ -93,6 +93,7 @@ def tile_routed_moe_kernel(tc, xT, w1, w2, gate, offs, out):
         w1q = {}
         w2q = {}
         hq = {}
+        gates = {}
 
         def quantize_w2(e, h, rows, shares, parts=1):
             grouped = grp.tile([P, N * PACK], BF16, name="grp_w2", bufs=4, align_bytes=64)
@@ -197,7 +198,7 @@ def tile_routed_moe_kernel(tc, xT, w1, w2, gate, offs, out):
             nc.vector.tensor_tensor(
                 window[b][:].indirect(offsets[:, e * C // 16 : (e + 1) * C // 16]),
                 y,
-                gate_last[:, b, :] if e == last else gate_sb[:, b, e * C : (e + 1) * C],
+                gates[e, b],
                 MULT,
             )
 
@@ -219,29 +220,44 @@ def tile_routed_moe_kernel(tc, xT, w1, w2, gate, offs, out):
             raw_w1 = [load(w1_v[e, g])[0] for g in range(G)]
             raw_w2 = load_w2(e)
             if e == 0:
-                nc.sync.dma_start(out=gate_sb[:], in_=gate_v[:, :, : last * C])
+                for b in range(NB):
+                    early = (last - b) * C
+                    nc.sync.dma_start(out=gate_sb[:, b, :early], in_=gate_v[:, b, :early])
+                    for i in range(last - b):
+                        gates[i, b] = gate_sb[:, b, i * C : (i + 1) * C]
             for g, shares in enumerate(((0, 96), (64, 64) if e < last - 1 else (80, 80))):
                 for h in range(HB):
                     prepare_half(e, g, h, by_columns(raw_w1[g][:, :, h * PASS : (h + 1) * PASS], shares[h]))
+            if e > 0:
+                finish(e - 1, 1, spent(raw_w1[1]))
             grouped_h = hid.tile([P, HB * half], BF16, name="grp_h", align_bytes=64)
             for h in range(HB):
                 layer1(e, h, grouped_h[:, h * half : (h + 1) * half], one_group=True)
             prepare_w2(e, raw_w2)
             for hs in ([range(HB)] if e < last - 1 else [[0], [1]]):
                 quantize_h(e, hs, grouped_h[:, hs[0] * half : (hs[-1] + 1) * half])
-            y = hid.tile([P, NB, C], F32, name="y")
-            for b in range(NB if e < last - 1 else 1):
-                finish(e, b, y[:, b : b + 1, :])
+            y = hid.tile([P, 1, C], F32, name="y")
+            finish(e, 0, y[:])
             if e == 1:
                 gather(4)
 
         first = load(w1_v[last, 0])[0]
         second = load(w1_v[last, 1][:, :, :PASS], w1_v[last, 1][:, :, PASS:])
-        *raw_w2, gate_last = load(*[w2_v[last, h] for h in range(HB)], gate_v[:, :, last * C :])
-        prepare_half(last, 0, 0, by_columns(first[:, :, :PASS], 32))
-        prepare_half(last, 0, 1, by_columns(first[:, :, PASS:], 80))
-        prepare_half(last, 1, 0, by_columns(second[0], 80))
-        grouped = copy_w1(1, by_columns(second[1], 84))
+        *raw_w2, late_1, late_0 = load(
+            *[w2_v[last, h] for h in range(HB)], gate_v[:, 1:, (last - 1) * C :], gate_v[:, :1, last * C :]
+        )
+        gates[last - 1, 1], gates[last, 1], gates[last, 0] = late_1[:, 0, :C], late_1[:, 0, C:], late_0[:, 0, :]
+        prepare_half(last, 0, 0, by_columns(first[:, :, :PASS], 48))
+        prepare_half(last, 0, 1, by_columns(first[:, :, PASS:], 48))
+        prepare_half(last, 1, 0, by_columns(second[0], 96))
+        grouped = copy_w1(
+            1,
+            [
+                (second[1], 0, 0, 2, on_vector),
+                (second[1][:, :, :160], 0, 2, PACK, on_vector),
+                (second[1][:, :, 160:], 40, 2, PACK, on_scalar),
+            ],
+        )
         quantize_w1(last, 1, 1, grouped, parts=PACK)
         last_h = hid.tile([P, half], BF16, name="grp_h", align_bytes=64)
         halves = (second[1][:, 0, PASS - half // 2 :].bitcast(BF16), last_h[:])

@@ -225,31 +225,35 @@ def tile_routed_moe_kernel(tc, xT, w1, w2, gate, offs, out):
                     nc.sync.dma_start(out=gate_sb[:, b, :early], in_=gate_v[:, b, :early])
                     for i in range(last - b):
                         gates[i, b] = gate_sb[:, b, i * C : (i + 1) * C]
-            for g, shares in enumerate(((0, 96), (64, 64) if e < last - 1 else (80, 80))):
-                for h in range(HB):
-                    prepare_half(e, g, h, by_columns(raw_w1[g][:, :, h * PASS : (h + 1) * PASS], shares[h]))
-            if e > 0:
-                finish(e - 1, 1, spent(raw_w1[1]))
+            for g in range(G):
+                low, high = raw_w1[g][:, :, :PASS], raw_w1[g][:, :, PASS:]
+                share = 80 if (e, g) == (last - 1, 1) else 64
+                prepare_half(e, g, 0, by_columns(low, share))
+                if e > 0 and (e, g) != (last - 1, 1):
+                    finish(e - 1, g, spent(low))
+                prepare_half(e, g, 1, by_columns(high, share))
             grouped_h = hid.tile([P, HB * half], BF16, name="grp_h", align_bytes=64)
             for h in range(HB):
                 layer1(e, h, grouped_h[:, h * half : (h + 1) * half], one_group=True)
             prepare_w2(e, raw_w2)
+            if e == last - 1:
+                finish(e - 1, 1, spent(raw_w2[1]))
             for hs in ([range(HB)] if e < last - 1 else [[0], [1]]):
                 quantize_h(e, hs, grouped_h[:, hs[0] * half : (hs[-1] + 1) * half])
-            y = hid.tile([P, 1, C], F32, name="y")
-            finish(e, 0, y[:])
             if e == 1:
                 gather(4)
 
+        y = hid.tile([P, 1, C], F32, name="y")
+        finish(last - 1, 0, y[:])
         first = load(w1_v[last, 0])[0]
         second = load(w1_v[last, 1][:, :, :PASS], w1_v[last, 1][:, :, PASS:])
         *raw_w2, late_1, late_0 = load(
             *[w2_v[last, h] for h in range(HB)], gate_v[:, 1:, (last - 1) * C :], gate_v[:, :1, last * C :]
         )
         gates[last - 1, 1], gates[last, 1], gates[last, 0] = late_1[:, 0, :C], late_1[:, 0, C:], late_0[:, 0, :]
-        prepare_half(last, 0, 0, by_columns(first[:, :, :PASS], 48))
+        prepare_half(last, 0, 0, by_columns(first[:, :, :PASS], 64))
         prepare_half(last, 0, 1, by_columns(first[:, :, PASS:], 48))
-        prepare_half(last, 1, 0, by_columns(second[0], 96))
+        prepare_half(last, 1, 0, by_columns(second[0], 88))
         grouped = copy_w1(
             1,
             [

@@ -41,16 +41,16 @@ def tile_routed_moe_kernel(tc, xT, w1, w2, gate, offs, out):
         psum_y = ctx.enter_context(tc.psum_pool(name="psum_y", bufs=4))
 
         offsets = keep.tile([P, E * C // 16], U16, name="offsets")
-        gate_sb = keep.tile([P, NB, (E - 1) * C], F32, name="gate_sb")
+        gate_sb = keep.tile([P, NB, (E - 1) * C], F32, name="gate_sb", align_bytes=256)
         xw = [keep.tile([P, T], U32, name=f"xw{g}", align_bytes=64) for g in range(G)]
         xs = [keep.tile([P, T], U8, name=f"xs{g}", align_bytes=64) for g in range(G)]
-        window = [keep.tile([P, T], F32, name=f"window{b}") for b in range(NB)]
+        window = [keep.tile([P, T], F32, name=f"window{b}", align_bytes=256) for b in range(NB)]
 
         for g in range(G):
             nc.gpsimd.memset(xs[g][:], 0)
 
         def load(*sources):
-            slot = staging.tile([P, PACK * H], F32, name="slot", align_bytes=64)
+            slot = staging.tile([P, PACK * H], F32, name="slot", align_bytes=256)
             views = []
             at = 0
             for src in sources:

@@ -43,11 +43,10 @@ def tile_routed_moe_kernel(tc, xT, w1, w2, gate, offs, out):
         offsets = keep.tile([P, E * C // 16], U16, name="offsets")
         gate_sb = keep.tile([P, NB, (E - 1) * C], F32, name="gate_sb", align_bytes=256)
         xw = [keep.tile([P, T], U32, name=f"xw{g}", align_bytes=64) for g in range(G)]
-        xs = [keep.tile([P, T], U8, name=f"xs{g}", align_bytes=64) for g in range(G)]
+        xs = keep.tile([P, T], U8, name="xs", align_bytes=64)
         window = [keep.tile([P, T], F32, name=f"window{b}", align_bytes=256) for b in range(NB)]
 
-        for g in range(G):
-            nc.gpsimd.memset(xs[g][:], 0)
+        nc.gpsimd.memset(xs[:], 0)
 
         def load(*sources):
             slot = staging.tile([P, PACK * H], F32, name="slot", align_bytes=256)
@@ -73,19 +72,19 @@ def tile_routed_moe_kernel(tc, xT, w1, w2, gate, offs, out):
             for t0, t1, copy in x_deal[g]:
                 grouped = grp.tile([P, (t1 - t0) * PACK], BF16, name=f"grp_x{t0}", align_bytes=64)
                 interleave(copy, grouped[:], raw_x[g][:, :, t0:t1])
-                nc.vector.quantize_mx(out=xw[g][:, t0:t1].bitcast(FP8X4), scales=xs[g][:, t0:t1], in_=grouped[:])
+                nc.vector.quantize_mx(out=xw[g][:, t0:t1].bitcast(FP8X4), scales=xs[PACK * g :, t0:t1], in_=grouped[:])
 
         xq = {}
 
         def gather(e0):
             gw = grp.tile([P, G, 2 * C], U32, name="gw", align_bytes=64)
-            gs = grp.tile([P, G, 2 * C], U8, name="gs", align_bytes=64)
+            gs = grp.tile([P, 2 * C], U8, name="gs", align_bytes=64)
             sl = offsets[:, e0 * C // 16 : (e0 + 2) * C // 16]
             for g in range(G):
                 nc.vector.tensor_copy(out=gw[:, g, :], in_=xw[g][:].indirect(sl))
-                nc.vector.tensor_copy(out=gs[:, g, :], in_=xs[g][:].indirect(sl))
                 for i in range(2):
-                    xq[e0 + i, g] = (gw[:, g, i * C : (i + 1) * C], gs[:, g, i * C : (i + 1) * C])
+                    xq[e0 + i, g] = (gw[:, g, i * C : (i + 1) * C], gs[PACK * g :, i * C : (i + 1) * C])
+            nc.vector.tensor_copy(out=gs[:], in_=xs[:].indirect(sl))
 
         gather(0)
         gather(2)
@@ -116,10 +115,10 @@ def tile_routed_moe_kernel(tc, xT, w1, w2, gate, offs, out):
         def copy_w1(h, shares, grouped=None):
             if grouped is None:
                 grouped = grp.tile([P, PASS * PACK], BF16, name=f"grp_w1_{h}", bufs=3, align_bytes=64)
-            dst = grouped[:].rearrange("p (t m j) -> p m j t", t=PACK, j=PACK)
+            dst = grouped[:].rearrange("p (t m u j) -> p m u t j", t=PACK, u=2, j=2)
             for rows, m0, t0, t1, copy in shares:
-                src = rows.rearrange("p j (m t) -> p m j t", t=PACK)
-                copy(out=dst[:, m0 : m0 + src.shape[1], :, t0:t1], in_=src[:, :, :, t0:t1])
+                src = rows.rearrange("p (u j) (m t) -> p m u t j", u=2, t=PACK)
+                copy(out=dst[:, m0 : m0 + src.shape[1], :, t0:t1, :], in_=src[:, :, :, t0:t1, :])
             return grouped
 
         def by_pairs(rows, m0=0):

@@ -61,8 +61,8 @@ def tile_routed_moe_kernel(tc, xT, w1, w2, gate, offs, out):
 
         def interleave(copy, dst, src):
             copy(
-                out=dst.rearrange("p (c i j) -> p c j i", i=4, j=PACK),
-                in_=src.rearrange("p j (c i) -> p c j i", i=4),
+                out=dst.rearrange("p (c i u j) -> p c u i j", i=4, u=2, j=2),
+                in_=src.rearrange("p (u j) (c i) -> p c u i j", u=2, i=4),
             )
 
         raw_x = [load(x_v[g])[0] for g in range(G)]

@@ -124,16 +124,14 @@ def tile_routed_moe_kernel(tc, xT, w1, w2, gate, offs, out):
         def by_pairs(rows, m0=0):
             return [(rows, m0, 0, 2, on_vector), (rows, m0, 2, 4, on_scalar)]
 
-        def quantize_w1(e, g, h, grouped, parts=1):
+        def quantize_w1(e, g, h, grouped, cuts=(0, PASS)):
             codes = cod.tile([P, PASS], U32, name="w1_codes", align_bytes=64)
             scales = cod.tile([P, PASS], U8, name="w1_scales", align_bytes=64)
-            width = PASS // parts
-            for c0 in range(0, PASS, width):
-                cols = slice(c0, c0 + width)
+            for c0, c1 in zip(cuts, cuts[1:]):
                 nc.vector.quantize_mx(
-                    out=codes[:, cols].bitcast(FP8X4),
-                    scales=scales[:, cols],
-                    in_=grouped[:, c0 * PACK : (c0 + width) * PACK],
+                    out=codes[:, c0:c1].bitcast(FP8X4),
+                    scales=scales[:, c0:c1],
+                    in_=grouped[:, c0 * PACK : c1 * PACK],
                 )
             w1q[e, g, h] = (codes, scales)
             return grouped
@@ -250,9 +248,9 @@ def tile_routed_moe_kernel(tc, xT, w1, w2, gate, offs, out):
             *[w2_v[last, h] for h in range(HB)], gate_v[:, 1:, (last - 1) * C :], gate_v[:, :1, last * C :]
         )
         gates[last - 1, 1], gates[last, 1], gates[last, 0] = late_1[:, 0, :C], late_1[:, 0, C:], late_0[:, 0, :]
-        prepare_half(last, 0, 0, by_columns(first[:, :, :PASS], 64))
+        prepare_half(last, 0, 0, by_columns(first[:, :, :PASS], 48))
         prepare_half(last, 0, 1, by_columns(first[:, :, PASS:], 48))
-        prepare_half(last, 1, 0, by_columns(second[0], 88))
+        prepare_half(last, 1, 0, by_columns(second[0], 80))
         grouped = copy_w1(
             1,
             [
@@ -261,7 +259,7 @@ def tile_routed_moe_kernel(tc, xT, w1, w2, gate, offs, out):
                 (second[1][:, :, 160:], 40, 2, PACK, on_scalar),
             ],
         )
-        quantize_w1(last, 1, 1, grouped, parts=PACK)
+        quantize_w1(last, 1, 1, grouped, cuts=(0, 2 * P, 3 * P, PASS))
         last_h = hid.tile([P, half], BF16, name="grp_h", align_bytes=64)
         halves = (second[1][:, 0, PASS - half // 2 :].bitcast(BF16), last_h[:])
         for h in range(HB):
@@ -273,20 +271,21 @@ def tile_routed_moe_kernel(tc, xT, w1, w2, gate, offs, out):
                 copy = on_scalar if (h, b) == (0, 1) else on_vector
                 interleave(copy, grouped[b][:, h, :], raw_w2[h][:, :, b * P : (b + 1) * P])
 
-        def quantize_block(b):
-            codes = hid.tile([P, HB, P], U32, name="w2_codes", bufs=8, align_bytes=64)
-            scales = hid.tile([P, HB, P], U8, name="w2_scales", bufs=8, align_bytes=64)
+        def quantize_block(b, h0, h1):
+            codes = hid.tile([P, h1 - h0, P], U32, name="w2_codes", bufs=8, align_bytes=64)
+            scales = hid.tile([P, h1 - h0, P], U8, name="w2_scales", bufs=8, align_bytes=64)
             nc.vector.quantize_mx(
                 out=codes[:].rearrange("p h c -> p (h c)").bitcast(FP8X4),
                 scales=scales[:].rearrange("p h c -> p (h c)"),
-                in_=grouped[b][:].rearrange("p h c -> p (h c)"),
+                in_=grouped[b][:, h0:h1, :].rearrange("p h c -> p (h c)"),
             )
-            for h in range(HB):
-                w2q[last, h, b] = (codes[:, h, :], scales[:, h, :])
+            for h in range(h0, h1):
+                w2q[last, h, b] = (codes[:, h - h0, :], scales[:, h - h0, :])
 
-        quantize_block(0)
+        quantize_block(0, 0, 1)
+        quantize_block(0, 1, 2)
         quantize_h(last, [1], halves[1])
-        quantize_block(1)
+        quantize_block(1, 0, 2)
         finish(last - 1, 1, raw_w2[1][:, :1, P:])
         for b in range(NB):
             finish(last, b, raw_w2[0][:, b : b + 1, :P])

@@ -20,6 +20,15 @@ PASS = P * PACK
 G = K // PASS
 HB = H // PASS
 NB = N // P
+LAST = E - 1
+LIST_ROWS = 16
+X_WIDE = 512
+PAIR = 2 * C
+
+EVEN = 64
+NO_SCATTER = 80
+LATE_START = 48
+LAST_HELP = 28
 
 
 def tile_routed_moe_kernel(tc, xT, w1, w2, gate, offs, out):
@@ -40,13 +49,13 @@ def tile_routed_moe_kernel(tc, xT, w1, w2, gate, offs, out):
         psum_a = ctx.enter_context(tc.psum_pool(name="psum_a", bufs=4))
         psum_y = ctx.enter_context(tc.psum_pool(name="psum_y", bufs=4))
 
-        offsets = keep.tile([P, E * C // 16], U16, name="offsets")
-        gate_sb = keep.tile([P, NB, (E - 1) * C], F32, name="gate_sb", align_bytes=256)
-        xw = [keep.tile([P, T], U32, name=f"xw{g}", align_bytes=64) for g in range(G)]
-        xs = keep.tile([P, T], U8, name="xs", align_bytes=64)
+        offsets = keep.tile([P, E * C // LIST_ROWS], U16, name="offsets")
+        gate_sb = keep.tile([P, NB, LAST * C], F32, name="gate_sb", align_bytes=256)
+        x_words = [keep.tile([P, T], U32, name=f"x_words{g}", align_bytes=64) for g in range(G)]
+        x_scales = keep.tile([P, T], U8, name="x_scales", align_bytes=64)
         window = [keep.tile([P, T], F32, name=f"window{b}", align_bytes=256) for b in range(NB)]
 
-        nc.gpsimd.memset(xs[:], 0)
+        nc.gpsimd.memset(x_scales[:], 0)
 
         def load(*sources):
             slot = staging.tile([P, PACK * H], F32, name="slot", align_bytes=256)
@@ -59,72 +68,50 @@ def tile_routed_moe_kernel(tc, xT, w1, w2, gate, offs, out):
                 at += size
             return views
 
-        def interleave(copy, dst, src):
+        def interleave(copy, dst, rows):
             copy(
-                out=dst.rearrange("p (c i u j) -> p c u i j", i=4, u=2, j=2),
-                in_=src.rearrange("p (u j) (c i) -> p c u i j", u=2, i=4),
+                out=dst.rearrange("p (c i u v) -> p c u i v", i=4, u=2, v=2),
+                in_=rows.rearrange("p (u v) (c i) -> p c u i v", u=2, i=4),
             )
+
+        def entries(first_slot, count):
+            return offsets[:, first_slot // LIST_ROWS : (first_slot + count) // LIST_ROWS]
 
         raw_x = [load(x_v[g])[0] for g in range(G)]
         nc.sync.dma_start(offsets[:], offs)
-        x_deal = (((0, 512, on_vector), (512, 768, on_scalar)), ((0, 512, on_scalar), (512, 768, on_vector)))
-        for g in range(G):
-            for t0, t1, copy in x_deal[g]:
+        for g, copies in enumerate(((on_vector, on_scalar), (on_scalar, on_vector))):
+            for (t0, t1), copy in zip(((0, X_WIDE), (X_WIDE, T)), copies):
                 grouped = grp.tile([P, (t1 - t0) * PACK], BF16, name=f"grp_x{t0}", align_bytes=64)
                 interleave(copy, grouped[:], raw_x[g][:, :, t0:t1])
-                nc.vector.quantize_mx(out=xw[g][:, t0:t1].bitcast(FP8X4), scales=xs[PACK * g :, t0:t1], in_=grouped[:])
+                nc.vector.quantize_mx(
+                    out=x_words[g][:, t0:t1].bitcast(FP8X4), scales=x_scales[PACK * g :, t0:t1], in_=grouped[:]
+                )
 
         xq = {}
-
-        def gather(e0):
-            gw = grp.tile([P, G, 2 * C], U32, name="gw", align_bytes=64)
-            gs = grp.tile([P, 2 * C], U8, name="gs", align_bytes=64)
-            sl = offsets[:, e0 * C // 16 : (e0 + 2) * C // 16]
-            for g in range(G):
-                nc.vector.tensor_copy(out=gw[:, g, :], in_=xw[g][:].indirect(sl))
-                for i in range(2):
-                    xq[e0 + i, g] = (gw[:, g, i * C : (i + 1) * C], gs[PACK * g :, i * C : (i + 1) * C])
-            nc.vector.tensor_copy(out=gs[:], in_=xs[:].indirect(sl))
-
-        gather(0)
-        gather(2)
-
         w1q = {}
         w2q = {}
         hq = {}
         gates = {}
 
-        def quantize_w2(e, h, rows, shares, parts=1):
-            grouped = grp.tile([P, N * PACK], BF16, name="grp_w2", bufs=4, align_bytes=64)
-            for c0, c1, copy in shares:
-                interleave(copy, grouped[:, c0 * PACK : c1 * PACK], rows[:, :, c0:c1])
-            codes = hid.tile([P, N], U32, name="w2_codes", bufs=8, align_bytes=64)
-            scales = hid.tile([P, N], U8, name="w2_scales", bufs=8, align_bytes=64)
-            width = N // parts
-            for c0 in range(0, N, width):
-                cols = slice(c0, c0 + width)
-                nc.vector.quantize_mx(
-                    out=codes[:, cols].bitcast(FP8X4),
-                    scales=scales[:, cols],
-                    in_=grouped[:, c0 * PACK : (c0 + width) * PACK],
-                )
-            for b in range(NB):
-                w2q[e, h, b] = (codes[:, b * P : (b + 1) * P], scales[:, b * P : (b + 1) * P])
-            return grouped
+        def gather(e0):
+            words = grp.tile([P, G, PAIR], U32, name="slot_words", align_bytes=64)
+            scales = grp.tile([P, PAIR], U8, name="slot_scales", align_bytes=64)
+            for g in range(G):
+                nc.vector.tensor_copy(out=words[:, g, :], in_=x_words[g][:].indirect(entries(e0 * C, PAIR)))
+                for i in range(PAIR // C):
+                    cols = slice(i * C, (i + 1) * C)
+                    xq[e0 + i, g] = (words[:, g, cols], scales[PACK * g :, cols])
+            nc.vector.tensor_copy(out=scales[:], in_=x_scales[:].indirect(entries(e0 * C, PAIR)))
 
-        def copy_w1(h, shares, grouped=None):
-            if grouped is None:
-                grouped = grp.tile([P, PASS * PACK], BF16, name=f"grp_w1_{h}", bufs=3, align_bytes=64)
-            dst = grouped[:].rearrange("p (t m u j) -> p m u t j", t=PACK, u=2, j=2)
+        def copy_w1(h, shares):
+            grouped = grp.tile([P, PASS * PACK], BF16, name=f"grp_w1_{h}", bufs=3, align_bytes=64)
+            dst = grouped[:].rearrange("p (t m u v) -> p m u t v", t=PACK, u=2, v=2)
             for rows, m0, t0, t1, copy in shares:
-                src = rows.rearrange("p (u j) (m t) -> p m u t j", u=2, t=PACK)
+                src = rows.rearrange("p (u v) (m t) -> p m u t v", u=2, t=PACK)
                 copy(out=dst[:, m0 : m0 + src.shape[1], :, t0:t1, :], in_=src[:, :, :, t0:t1, :])
             return grouped
 
-        def by_pairs(rows, m0=0):
-            return [(rows, m0, 0, 2, on_vector), (rows, m0, 2, 4, on_scalar)]
-
-        def quantize_w1(e, g, h, grouped, cuts=(0, PASS)):
+        def quantize_w1(e, g, h, grouped, cuts):
             codes = cod.tile([P, PASS], U32, name="w1_codes", align_bytes=64)
             scales = cod.tile([P, PASS], U8, name="w1_scales", align_bytes=64)
             for c0, c1 in zip(cuts, cuts[1:]):
@@ -134,35 +121,28 @@ def tile_routed_moe_kernel(tc, xT, w1, w2, gate, offs, out):
                     in_=grouped[:, c0 * PACK : c1 * PACK],
                 )
             w1q[e, g, h] = (codes, scales)
-            return grouped
 
-        def by_columns(rows, m1):
-            shares = [(rows[:, :, : m1 * PACK], 0, 0, PACK, on_vector), (rows[:, :, m1 * PACK :], m1, 0, PACK, on_scalar)]
-            return [share for share in shares if share[0].shape[2]]
+        def prepare_half(e, g, h, rows, share):
+            shares = [
+                (rows[:, :, : share * PACK], 0, 0, PACK, on_vector),
+                (rows[:, :, share * PACK :], share, 0, PACK, on_scalar),
+            ]
+            quantize_w1(e, g, h, copy_w1(h, shares), (0, PASS))
 
-        def prepare_half(e, g, h, shares):
-            return quantize_w1(e, g, h, copy_w1(h, shares))
-
-        def spent(rows):
-            return rows[:, :1, :C]
-
-        def layer1(e, h, grouped, one_group=False):
+        def layer1(e, h, grouped):
             acc = psum_a.tile([P, PACK, C], F32, name="acc_a")
-            if one_group:
-                passes = [(t, g, (g, t) == (0, 0), (g, t) == (G - 1, PACK - 1)) for g in range(G) for t in range(PACK)]
-            else:
-                passes = [(t, g, g == 0, g == G - 1) for t in range(PACK) for g in range(G)]
-            for t, g, start, stop in passes:
+            for g in range(G):
                 codes, scales = w1q[e, g, h]
-                nc.tensor.matmul_mx(
-                    out=acc[:, t, :],
-                    lhsT=codes[:, t * P : (t + 1) * P].bitcast(FP8X4),
-                    lhsT_scale=scales[:, t * P : (t + 1) * P],
-                    rhs=xq[e, g][0].bitcast(FP8X4),
-                    rhs_scale=xq[e, g][1],
-                    start=start,
-                    stop=stop,
-                )
+                for t in range(PACK):
+                    nc.tensor.matmul_mx(
+                        out=acc[:, t, :],
+                        lhsT=codes[:, t * P : (t + 1) * P].bitcast(FP8X4),
+                        lhsT_scale=scales[:, t * P : (t + 1) * P],
+                        rhs=xq[e, g][0].bitcast(FP8X4),
+                        rhs_scale=xq[e, g][1],
+                        start=(g, t) == (0, 0),
+                        stop=(g, t) == (G - 1, PACK - 1),
+                    )
             nc.scalar.activation(
                 grouped.rearrange("p (n t) -> p n t", t=PACK),
                 acc[:].rearrange("p t n -> p n t"),
@@ -176,117 +156,114 @@ def tile_routed_moe_kernel(tc, xT, w1, w2, gate, offs, out):
             for i, h in enumerate(hs):
                 hq[e, h] = (codes[:, i * C : (i + 1) * C], scales[:, i * C : (i + 1) * C])
 
-        def layer2(e, bs, room):
-            acc = psum_y.tile([P, len(bs), C], F32, name="acc_y")
-            for i, b in enumerate(bs):
-                for h in range(HB):
-                    nc.tensor.matmul_mx(
-                        out=acc[:, i, :],
-                        lhsT=w2q[e, h, b][0].bitcast(FP8X4),
-                        lhsT_scale=w2q[e, h, b][1],
-                        rhs=hq[e, h][0].bitcast(FP8X4),
-                        rhs_scale=hq[e, h][1],
-                        start=(h == 0),
-                        stop=(h == HB - 1),
-                    )
-            nc.scalar.copy(out=room, in_=acc[:])
+        def quantize_w2(grouped):
+            width = grouped.shape[1] // PACK
+            codes = hid.tile([P, width], U32, name="w2_codes", bufs=8, align_bytes=64)
+            scales = hid.tile([P, width], U8, name="w2_scales", bufs=8, align_bytes=64)
+            nc.vector.quantize_mx(out=codes[:].bitcast(FP8X4), scales=scales[:], in_=grouped)
+            return [(codes[:, c0 : c0 + P], scales[:, c0 : c0 + P]) for c0 in range(0, width, P)]
 
-        def scatter(e, b, y):
-            nc.vector.tensor_tensor(
-                window[b][:].indirect(offsets[:, e * C // 16 : (e + 1) * C // 16]),
-                y,
-                gates[e, b],
-                MULT,
-            )
+        def prepare_w2(e, passes):
+            for h, copy in enumerate((on_scalar, on_vector)):
+                grouped = grp.tile([P, N * PACK], BF16, name="grp_w2", bufs=4, align_bytes=64)
+                interleave(copy, grouped[:], passes[h])
+                for b, block in enumerate(quantize_w2(grouped[:])):
+                    w2q[e, h, b] = block
 
         def finish(e, b, room):
-            layer2(e, [b], room)
-            scatter(e, b, room[:, 0, :])
+            acc = psum_y.tile([P, C], F32, name="acc_y")
+            for h in range(HB):
+                nc.tensor.matmul_mx(
+                    out=acc[:],
+                    lhsT=w2q[e, h, b][0].bitcast(FP8X4),
+                    lhsT_scale=w2q[e, h, b][1],
+                    rhs=hq[e, h][0].bitcast(FP8X4),
+                    rhs_scale=hq[e, h][1],
+                    start=(h == 0),
+                    stop=(h == HB - 1),
+                )
+            nc.scalar.copy(out=room, in_=acc[:])
+            nc.vector.tensor_tensor(window[b][:].indirect(entries(e * C, C)), room, gates[e, b], MULT)
 
-        def load_w2(e):
-            raw = load(w2[e].rearrange("(h p j) c -> p h (j c)", p=P, j=PACK))[0]
-            return [raw[:, h, :].rearrange("p (j c) -> p j c", j=PACK) for h in range(HB)]
+        gather(0)
+        gather(2)
 
-        def prepare_w2(e, raw):
-            for h, copy in enumerate((on_scalar, on_vector)):
-                quantize_w2(e, h, raw[h], [(0, N, copy)])
-
-        last = E - 1
         half = C * PACK
-        for e in range(last):
+        for e in range(LAST):
             raw_w1 = [load(w1_v[e, g])[0] for g in range(G)]
-            raw_w2 = load_w2(e)
+            both = load(w2[e].rearrange("(h p j) c -> p h (j c)", p=P, j=PACK))[0]
+            raw_w2 = [both[:, h, :].rearrange("p (j c) -> p j c", j=PACK) for h in range(HB)]
             if e == 0:
                 for b in range(NB):
-                    early = (last - b) * C
-                    nc.sync.dma_start(out=gate_sb[:, b, :early], in_=gate_v[:, b, :early])
-                    for i in range(last - b):
+                    early = LAST - b
+                    nc.sync.dma_start(out=gate_sb[:, b, : early * C], in_=gate_v[:, b, : early * C])
+                    for i in range(early):
                         gates[i, b] = gate_sb[:, b, i * C : (i + 1) * C]
             for g in range(G):
                 low, high = raw_w1[g][:, :, :PASS], raw_w1[g][:, :, PASS:]
-                share = 80 if (e, g) == (last - 1, 1) else 64
-                prepare_half(e, g, 0, by_columns(low, share))
-                if e > 0 and (e, g) != (last - 1, 1):
-                    finish(e - 1, g, spent(low))
-                prepare_half(e, g, 1, by_columns(high, share))
+                scatter_here = e > 0 and (e, g) != (LAST - 1, 1)
+                share = NO_SCATTER if (e, g) == (LAST - 1, 1) else EVEN
+                prepare_half(e, g, 0, low, share)
+                if scatter_here:
+                    finish(e - 1, g, low[:, 0, :C])
+                prepare_half(e, g, 1, high, share)
             grouped_h = hid.tile([P, HB * half], BF16, name="grp_h", align_bytes=64)
-            for h in range(HB):
-                layer1(e, h, grouped_h[:, h * half : (h + 1) * half], one_group=True)
-            prepare_w2(e, raw_w2)
-            if e == last - 1:
-                finish(e - 1, 1, spent(raw_w2[1]))
-            for hs in ([range(HB)] if e < last - 1 else [[0], [1]]):
-                quantize_h(e, hs, grouped_h[:, hs[0] * half : (hs[-1] + 1) * half])
+            if e < LAST - 1:
+                for h in range(HB):
+                    layer1(e, h, grouped_h[:, h * half : (h + 1) * half])
+                prepare_w2(e, raw_w2)
+                quantize_h(e, range(HB), grouped_h[:])
+            else:
+                prepare_w2(e, raw_w2)
+                halves = (raw_w2[0][:, 0, :].bitcast(BF16), grouped_h[:, half:])
+                for h in range(HB):
+                    layer1(e, h, halves[h])
+                for h in range(HB):
+                    quantize_h(e, [h], halves[h])
+                finish(e - 1, 1, raw_w2[0][:, 0, :C])
             if e == 1:
                 gather(4)
 
-        y = hid.tile([P, 1, C], F32, name="y")
-        finish(last - 1, 0, y[:])
-        first = load(w1_v[last, 0])[0]
-        second = load(w1_v[last, 1][:, :, :PASS], w1_v[last, 1][:, :, PASS:])
+        y = hid.tile([P, C], F32, name="y")
+        finish(LAST - 1, 0, y[:])
+
+        first = load(w1_v[LAST, 0])[0]
+        low, high = load(w1_v[LAST, 1][:, :, :PASS], w1_v[LAST, 1][:, :, PASS:])
         *raw_w2, late_1, late_0 = load(
-            *[w2_v[last, h] for h in range(HB)], gate_v[:, 1:, (last - 1) * C :], gate_v[:, :1, last * C :]
+            *[w2_v[LAST, h] for h in range(HB)], gate_v[:, 1:, (LAST - 1) * C :], gate_v[:, :1, LAST * C :]
         )
-        gates[last - 1, 1], gates[last, 1], gates[last, 0] = late_1[:, 0, :C], late_1[:, 0, C:], late_0[:, 0, :]
-        prepare_half(last, 0, 0, by_columns(first[:, :, :PASS], 48))
-        prepare_half(last, 0, 1, by_columns(first[:, :, PASS:], 48))
-        prepare_half(last, 1, 0, by_columns(second[0], 80))
+        gates[LAST - 1, 1], gates[LAST, 1], gates[LAST, 0] = late_1[:, 0, :C], late_1[:, 0, C:], late_0[:, 0, :]
+        prepare_half(LAST, 0, 0, first[:, :, :PASS], LATE_START)
+        prepare_half(LAST, 0, 1, first[:, :, PASS:], LATE_START)
+        prepare_half(LAST, 1, 0, low, NO_SCATTER)
+        pair = PACK // 2
         grouped = copy_w1(
             1,
             [
-                (second[1], 0, 0, 2, on_vector),
-                (second[1][:, :, :160], 0, 2, PACK, on_vector),
-                (second[1][:, :, 160:], 40, 2, PACK, on_scalar),
+                (high, 0, 0, pair, on_vector),
+                (high[:, :, : LAST_HELP * PACK], 0, pair, PACK, on_vector),
+                (high[:, :, LAST_HELP * PACK :], LAST_HELP, pair, PACK, on_scalar),
             ],
         )
-        quantize_w1(last, 1, 1, grouped, cuts=(0, 2 * P, 3 * P, PASS))
+        quantize_w1(LAST, 1, 1, grouped, (0, 2 * P, 3 * P, PASS))
         last_h = hid.tile([P, half], BF16, name="grp_h", align_bytes=64)
-        halves = (second[1][:, 0, PASS - half // 2 :].bitcast(BF16), last_h[:])
+        halves = (high[:, 0, PASS - half // 2 :].bitcast(BF16), last_h[:])
         for h in range(HB):
-            layer1(last, h, halves[h], one_group=True)
-        quantize_h(last, [0], halves[0])
-        grouped = [grp.tile([P, HB, P * PACK], BF16, name="grp_w2", bufs=4, align_bytes=64) for b in range(NB)]
+            layer1(LAST, h, halves[h])
+        quantize_h(LAST, [0], halves[0])
+
+        blocks = [grp.tile([P, HB, P * PACK], BF16, name="grp_w2", bufs=4, align_bytes=64) for b in range(NB)]
         for h in range(HB):
             for b in range(NB):
                 copy = on_scalar if (h, b) == (0, 1) else on_vector
-                interleave(copy, grouped[b][:, h, :], raw_w2[h][:, :, b * P : (b + 1) * P])
+                interleave(copy, blocks[b][:, h, :], raw_w2[h][:, :, b * P : (b + 1) * P])
+        for h in range(HB):
+            w2q[LAST, h, 0] = quantize_w2(blocks[0][:, h, :])[0]
+        quantize_h(LAST, [1], halves[1])
+        for h, block in enumerate(quantize_w2(blocks[1][:].rearrange("p h c -> p (h c)"))):
+            w2q[LAST, h, 1] = block
 
-        def quantize_block(b, h0, h1):
-            codes = hid.tile([P, h1 - h0, P], U32, name="w2_codes", bufs=8, align_bytes=64)
-            scales = hid.tile([P, h1 - h0, P], U8, name="w2_scales", bufs=8, align_bytes=64)
-            nc.vector.quantize_mx(
-                out=codes[:].rearrange("p h c -> p (h c)").bitcast(FP8X4),
-                scales=scales[:].rearrange("p h c -> p (h c)"),
-                in_=grouped[b][:, h0:h1, :].rearrange("p h c -> p (h c)"),
-            )
-            for h in range(h0, h1):
-                w2q[last, h, b] = (codes[:, h - h0, :], scales[:, h - h0, :])
-
-        quantize_block(0, 0, 1)
-        quantize_block(0, 1, 2)
-        quantize_h(last, [1], halves[1])
-        quantize_block(1, 0, 2)
-        finish(last - 1, 1, raw_w2[1][:, :1, P:])
+        finish(LAST - 1, 1, raw_w2[1][:, 0, P:])
         for b in range(NB):
-            finish(last, b, raw_w2[0][:, b : b + 1, :P])
+            finish(LAST, b, raw_w2[0][:, b, :P])
             nc.sync.dma_start(out=out_v[b], in_=window[b][:])

@@ -108,7 +108,10 @@ def tile_routed_moe_kernel(tc, xT, w1, w2, gate, offs, out):
             dst = grouped[:].rearrange("p (t m u v) -> p m u t v", t=PACK, u=2, v=2)
             for rows, m0, t0, t1, copy in shares:
                 src = rows.rearrange("p (u v) (m t) -> p m u t v", u=2, t=PACK)
-                copy(out=dst[:, m0 : m0 + src.shape[1], :, t0:t1, :], in_=src[:, :, :, t0:t1, :])
+                a, b = dst[:, m0 : m0 + src.shape[1], :, t0:t1, :], src[:, :, :, t0:t1, :]
+                if t1 - t0 < PACK:
+                    a, b = a.rearrange("p m u t v -> p m u v t"), b.rearrange("p m u t v -> p m u v t")
+                copy(out=a, in_=b)
             return grouped
 
         def quantize_w1(e, g, h, grouped, cuts):

@@ -68,6 +68,14 @@ def tile_routed_moe_kernel(tc, xT, w1, w2, gate, offs, out):
                 at += size
             return views
 
+        def load_by_pairs(src):
+            slot = staging.tile([P, PACK * H], F32, name="slot", align_bytes=256)
+            view = slot[:, : src.shape[1] * src.shape[2]].rearrange("p (r c) -> p r c", r=src.shape[1])
+            mid = src.shape[1] // 2
+            nc.sync.dma_start(out=view[:, :mid], in_=src[:, :mid])
+            nc.sync.dma_start(out=view[:, mid:], in_=src[:, mid:])
+            return view
+
         def interleave(copy, dst, rows):
             copy(
                 out=dst.rearrange("p (c i u v) -> p c u i v", i=4, u=2, v=2),
@@ -193,8 +201,8 @@ def tile_routed_moe_kernel(tc, xT, w1, w2, gate, offs, out):
 
         half = C * PACK
         for e in range(LAST):
-            raw_w1 = [load(w1_v[e, g])[0] for g in range(G)]
-            both = load(w2[e].rearrange("(h p j) c -> p h (j c)", p=P, j=PACK))[0]
+            raw_w1 = [load_by_pairs(w1_v[e, g]) if e < 3 else load(w1_v[e, g])[0] for g in range(G)]
+            both = load_by_pairs(w2[e].rearrange("(h p j) c -> p h (j c)", p=P, j=PACK))
             raw_w2 = [both[:, h, :].rearrange("p (j c) -> p j c", j=PACK) for h in range(HB)]
             if e == 0:
                 for b in range(NB):

@@ -68,14 +68,6 @@ def tile_routed_moe_kernel(tc, xT, w1, w2, gate, offs, out):
                 at += size
             return views
 
-        def load_by_pairs(src):
-            slot = staging.tile([P, PACK * H], F32, name="slot", align_bytes=256)
-            view = slot[:, : src.shape[1] * src.shape[2]].rearrange("p (r c) -> p r c", r=src.shape[1])
-            mid = src.shape[1] // 2
-            nc.sync.dma_start(out=view[:, :mid], in_=src[:, :mid])
-            nc.sync.dma_start(out=view[:, mid:], in_=src[:, mid:])
-            return view
-
         def interleave(copy, dst, rows):
             copy(
                 out=dst.rearrange("p (c i u v) -> p c u i v", i=4, u=2, v=2),
@@ -201,9 +193,8 @@ def tile_routed_moe_kernel(tc, xT, w1, w2, gate, offs, out):
 
         half = C * PACK
         for e in range(LAST):
-            raw_w1 = [load_by_pairs(w1_v[e, g]) if e < 3 else load(w1_v[e, g])[0] for g in range(G)]
-            both = load_by_pairs(w2[e].rearrange("(h p j) c -> p h (j c)", p=P, j=PACK))
-            raw_w2 = [both[:, h, :].rearrange("p (j c) -> p j c", j=PACK) for h in range(HB)]
+            raw_w1 = [load(w1_v[e, g])[0] for g in range(G)]
+            raw_w2 = load(*[w2_v[e, h] for h in range(HB)])
             if e == 0:
                 for b in range(NB):
                     early = LAST - b

@@ -23,9 +23,8 @@ NB = N // P
 LAST = E - 1
 LIST_ROWS = 16
 X_WIDE = 512
-PAIR = 2 * C
+GATHER = E * C // 2
 
-EVEN = 64
 NO_SCATTER = 80
 LATE_START = 48
 LAST_HELP = 28
@@ -93,15 +92,15 @@ def tile_routed_moe_kernel(tc, xT, w1, w2, gate, offs, out):
         hq = {}
         gates = {}
 
-        def gather(e0):
-            words = grp.tile([P, G, PAIR], U32, name="slot_words", align_bytes=64)
-            scales = grp.tile([P, PAIR], U8, name="slot_scales", align_bytes=64)
+        slot_words = keep.tile([P, G, E * C], U32, name="slot_words", align_bytes=64)
+        slot_scales = keep.tile([P, E * C], U8, name="slot_scales", align_bytes=64)
+        for s0 in range(0, E * C, GATHER):
             for g in range(G):
-                nc.vector.tensor_copy(out=words[:, g, :], in_=x_words[g][:].indirect(entries(e0 * C, PAIR)))
-                for i in range(PAIR // C):
-                    cols = slice(i * C, (i + 1) * C)
-                    xq[e0 + i, g] = (words[:, g, cols], scales[PACK * g :, cols])
-            nc.vector.tensor_copy(out=scales[:], in_=x_scales[:].indirect(entries(e0 * C, PAIR)))
+                on_vector(out=slot_words[:, g, s0 : s0 + GATHER], in_=x_words[g][:].indirect(entries(s0, GATHER)))
+            on_vector(out=slot_scales[:, s0 : s0 + GATHER], in_=x_scales[:].indirect(entries(s0, GATHER)))
+        for e in range(E):
+            for g in range(G):
+                xq[e, g] = (slot_words[:, g, e * C : (e + 1) * C], slot_scales[PACK * g :, e * C : (e + 1) * C])
 
         def copy_w1(h, shares):
             grouped = grp.tile([P, PASS * PACK], BF16, name=f"grp_w1_{h}", bufs=3, align_bytes=64)
@@ -127,9 +126,10 @@ def tile_routed_moe_kernel(tc, xT, w1, w2, gate, offs, out):
 
         def prepare_half(e, g, h, rows, share):
             shares = [
-                (rows[:, :, : share * PACK], 0, 0, PACK, on_vector),
-                (rows[:, :, share * PACK :], share, 0, PACK, on_scalar),
+                (0, share, on_vector),
+                (share, P, on_scalar),
             ]
+            shares = [(rows[:, :, m0 * PACK : m1 * PACK], m0, 0, PACK, copy) for m0, m1, copy in shares if m1 > m0]
             quantize_w1(e, g, h, copy_w1(h, shares), (0, PASS))
 
         def layer1(e, h, grouped):
@@ -161,17 +161,17 @@ def tile_routed_moe_kernel(tc, xT, w1, w2, gate, offs, out):
 
         def quantize_w2(grouped):
             width = grouped.shape[1] // PACK
-            codes = hid.tile([P, width], U32, name="w2_codes", bufs=8, align_bytes=64)
-            scales = hid.tile([P, width], U8, name="w2_scales", bufs=8, align_bytes=64)
+            codes = hid.tile([P, width], U32, name="w2_codes", bufs=5, align_bytes=64)
+            scales = hid.tile([P, width], U8, name="w2_scales", bufs=5, align_bytes=64)
             nc.vector.quantize_mx(out=codes[:].bitcast(FP8X4), scales=scales[:], in_=grouped)
             return [(codes[:, c0 : c0 + P], scales[:, c0 : c0 + P]) for c0 in range(0, width, P)]
 
         def prepare_w2(e, passes):
+            grouped = grp.tile([P, HB, N * PACK], BF16, name="grp_w2", bufs=2, align_bytes=64)
             for h, copy in enumerate((on_scalar, on_vector)):
-                grouped = grp.tile([P, N * PACK], BF16, name="grp_w2", bufs=4, align_bytes=64)
-                interleave(copy, grouped[:], passes[h])
-                for b, block in enumerate(quantize_w2(grouped[:])):
-                    w2q[e, h, b] = block
+                interleave(copy, grouped[:, h, :], passes[h])
+            for i, block in enumerate(quantize_w2(grouped[:].rearrange("p h c -> p (h c)"))):
+                w2q[e, i // NB, i % NB] = block
 
         def finish(e, b, room):
             acc = psum_y.tile([P, C], F32, name="acc_y")
@@ -188,9 +188,6 @@ def tile_routed_moe_kernel(tc, xT, w1, w2, gate, offs, out):
             nc.scalar.copy(out=room, in_=acc[:])
             nc.vector.tensor_tensor(window[b][:].indirect(entries(e * C, C)), room, gates[e, b], MULT)
 
-        gather(0)
-        gather(2)
-
         half = C * PACK
         for e in range(LAST):
             raw_w1 = [load(w1_v[e, g])[0] for g in range(G)]
@@ -204,11 +201,11 @@ def tile_routed_moe_kernel(tc, xT, w1, w2, gate, offs, out):
             for g in range(G):
                 low, high = raw_w1[g][:, :, :PASS], raw_w1[g][:, :, PASS:]
                 scatter_here = e > 0 and (e, g) != (LAST - 1, 1)
-                share = NO_SCATTER if (e, g) == (LAST - 1, 1) else EVEN
-                prepare_half(e, g, 0, low, share)
+                shares = (NO_SCATTER, NO_SCATTER) if (e, g) == (LAST - 1, 1) else (P, 0)
+                prepare_half(e, g, 0, low, shares[0])
                 if scatter_here:
                     finish(e - 1, g, low[:, 0, :C])
-                prepare_half(e, g, 1, high, share)
+                prepare_half(e, g, 1, high, shares[1])
             grouped_h = hid.tile([P, HB * half], BF16, name="grp_h", align_bytes=64)
             if e < LAST - 1:
                 for h in range(HB):
@@ -223,8 +220,6 @@ def tile_routed_moe_kernel(tc, xT, w1, w2, gate, offs, out):
                 for h in range(HB):
                     quantize_h(e, [h], halves[h])
                 finish(e - 1, 1, raw_w2[0][:, 0, :C])
-            if e == 1:
-                gather(4)
 
         y = hid.tile([P, C], F32, name="y")
         finish(LAST - 1, 0, y[:])
@@ -254,7 +249,7 @@ def tile_routed_moe_kernel(tc, xT, w1, w2, gate, offs, out):
             layer1(LAST, h, halves[h])
         quantize_h(LAST, [0], halves[0])
 
-        blocks = [grp.tile([P, HB, P * PACK], BF16, name="grp_w2", bufs=4, align_bytes=64) for b in range(NB)]
+        blocks = [grp.tile([P, HB, P * PACK], BF16, name="grp_w2", bufs=2, align_bytes=64) for b in range(NB)]
         for h in range(HB):
             for b in range(NB):
                 copy = on_scalar if (h, b) == (0, 1) else on_vector

@@ -191,7 +191,11 @@ def tile_routed_moe_kernel(tc, xT, w1, w2, gate, offs, out):
         half = C * PACK
         for e in range(LAST):
             raw_w1 = [load(w1_v[e, g])[0] for g in range(G)]
-            raw_w2 = load(*[w2_v[e, h] for h in range(HB)])
+            if e == LAST - 1:
+                raw_w2 = load(*[w2_v[e, h] for h in range(HB)])
+            else:
+                both = load(w2[e].rearrange("(h p j) c -> p h (j c)", p=P, j=PACK))[0]
+                raw_w2 = [both[:, h, :].rearrange("p (j c) -> p j c", j=PACK) for h in range(HB)]
             if e == 0:
                 for b in range(NB):
                     early = LAST - b

@@ -191,7 +191,7 @@ def tile_routed_moe_kernel(tc, xT, w1, w2, gate, offs, out):
         half = C * PACK
         for e in range(LAST):
             raw_w1 = [load(w1_v[e, g])[0] for g in range(G)]
-            if e == LAST - 1:
+            if e >= 2:
                 raw_w2 = load(*[w2_v[e, h] for h in range(HB)])
             else:
                 both = load(w2[e].rearrange("(h p j) c -> p h (j c)", p=P, j=PACK))[0]

@@ -23,10 +23,12 @@ NB = N // P
 LAST = E - 1
 LIST_ROWS = 16
 X_WIDE = 512
+SHIFT = 2
 GATHER = E * C // 2
 
 NO_SCATTER = 80
 LATE_START = 48
+LAST_LOW = 96
 LAST_HELP = 28
 
 
@@ -204,11 +206,11 @@ def tile_routed_moe_kernel(tc, xT, w1, w2, gate, offs, out):
                         gates[i, b] = gate_sb[:, b, i * C : (i + 1) * C]
             for g in range(G):
                 low, high = raw_w1[g][:, :, :PASS], raw_w1[g][:, :, PASS:]
-                scatter_here = e > 0 and (e, g) != (LAST - 1, 1)
+                scatter_here = 0 < e <= SHIFT or (e > SHIFT and g == 0)
                 shares = (NO_SCATTER, NO_SCATTER) if (e, g) == (LAST - 1, 1) else (P, 0)
                 prepare_half(e, g, 0, low, shares[0])
                 if scatter_here:
-                    finish(e - 1, g, low[:, 0, :C])
+                    finish(e - 1, g if e <= SHIFT else 1, low[:, 0, :C])
                 prepare_half(e, g, 1, high, shares[1])
             grouped_h = hid.tile([P, HB * half], BF16, name="grp_h", align_bytes=64)
             if e < LAST - 1:
@@ -223,10 +225,9 @@ def tile_routed_moe_kernel(tc, xT, w1, w2, gate, offs, out):
                     layer1(e, h, halves[h])
                 for h in range(HB):
                     quantize_h(e, [h], halves[h])
-                finish(e - 1, 1, raw_w2[0][:, 0, :C])
-
-        y = hid.tile([P, C], F32, name="y")
-        finish(LAST - 1, 0, y[:])
+            if e >= SHIFT:
+                y = hid.tile([P, C], F32, name="y")
+                finish(e, 0, y[:])
 
         first = load(w1_v[LAST, 0])[0]
         low, high = load(w1_v[LAST, 1][:, :, :PASS], w1_v[LAST, 1][:, :, PASS:])
@@ -236,7 +237,7 @@ def tile_routed_moe_kernel(tc, xT, w1, w2, gate, offs, out):
         gates[LAST - 1, 1], gates[LAST, 1], gates[LAST, 0] = late_1[:, 0, :C], late_1[:, 0, C:], late_0[:, 0, :]
         prepare_half(LAST, 0, 0, first[:, :, :PASS], LATE_START)
         prepare_half(LAST, 0, 1, first[:, :, PASS:], LATE_START)
-        prepare_half(LAST, 1, 0, low, NO_SCATTER)
+        prepare_half(LAST, 1, 0, low, LAST_LOW)
         pair = PACK // 2
         grouped = copy_w1(
             1,

@@ -58,16 +58,15 @@ def tile_routed_moe_kernel(tc, xT, w1, w2, gate, offs, out):
 
         nc.gpsimd.memset(x_scales[:], 0)
 
-        def load(*sources):
+        def load(*sources, at=0):
             slot = staging.tile([P, PACK * H], F32, name="slot", align_bytes=256)
             views = []
-            at = 0
             for src in sources:
                 size = src.shape[1] * src.shape[2]
                 views.append(slot[:, at : at + size].rearrange("p (r c) -> p r c", r=src.shape[1]))
                 nc.sync.dma_start(out=views[-1], in_=src)
                 at += size
-            return views
+            return views + [slot]
 
         def interleave(copy, dst, rows):
             copy(
@@ -126,13 +125,13 @@ def tile_routed_moe_kernel(tc, xT, w1, w2, gate, offs, out):
                 )
             w1q[e, g, h] = (codes, scales)
 
-        def prepare_half(e, g, h, rows, share):
+        def prepare_half(e, g, h, rows, share, cuts=(0, PASS)):
             shares = [
                 (0, share, on_vector),
                 (share, P, on_scalar),
             ]
             shares = [(rows[:, :, m0 * PACK : m1 * PACK], m0, 0, PACK, copy) for m0, m1, copy in shares if m1 > m0]
-            quantize_w1(e, g, h, copy_w1(h, shares), (0, PASS))
+            quantize_w1(e, g, h, copy_w1(h, shares), cuts)
 
         def layer1(e, h, grouped):
             acc = psum_a.tile([P, PACK, C], F32, name="acc_a")
@@ -194,7 +193,7 @@ def tile_routed_moe_kernel(tc, xT, w1, w2, gate, offs, out):
         for e in range(LAST):
             raw_w1 = [load(w1_v[e, g])[0] for g in range(G)]
             if e >= 2:
-                raw_w2 = load(*[w2_v[e, h] for h in range(HB)])
+                *raw_w2, slot_w2 = load(*[w2_v[e, h] for h in range(HB)], at=P)
             else:
                 both = load(w2[e].rearrange("(h p j) c -> p h (j c)", p=P, j=PACK))[0]
                 raw_w2 = [both[:, h, :].rearrange("p (j c) -> p j c", j=PACK) for h in range(HB)]
@@ -211,7 +210,7 @@ def tile_routed_moe_kernel(tc, xT, w1, w2, gate, offs, out):
                 prepare_half(e, g, 0, low, shares[0])
                 if scatter_here:
                     finish(e - 1, g if e <= SHIFT else 1, low[:, 0, :C])
-                prepare_half(e, g, 1, high, shares[1])
+                prepare_half(e, g, 1, high, shares[1], (0, 2 * P, PASS) if (e, g) == (LAST - 1, 1) else (0, PASS))
             grouped_h = hid.tile([P, HB * half], BF16, name="grp_h", align_bytes=64)
             if e < LAST - 1:
                 for h in range(HB):
@@ -219,21 +218,30 @@ def tile_routed_moe_kernel(tc, xT, w1, w2, gate, offs, out):
                 prepare_w2(e, raw_w2)
                 quantize_h(e, range(HB), grouped_h[:])
             else:
-                prepare_w2(e, raw_w2)
-                halves = (raw_w2[0][:, 0, :].bitcast(BF16), grouped_h[:, half:])
+                blocks = [grp.tile([P, HB, P * PACK], BF16, name="grp_w2", bufs=2, align_bytes=64) for b in range(NB)]
+
+                def prepare_block(b):
+                    for h, copy in enumerate((on_scalar, on_vector)):
+                        interleave(copy, blocks[b][:, h, :], raw_w2[h][:, :, b * P : (b + 1) * P])
+                    for h, block in enumerate(quantize_w2(blocks[b][:].rearrange("p h c -> p (h c)"))):
+                        w2q[e, h, b] = block
+
+                prepare_block(0)
+                halves = (slot_w2[:, : half // 2].bitcast(BF16), grouped_h[:, half:])
                 for h in range(HB):
                     layer1(e, h, halves[h])
                 for h in range(HB):
                     quantize_h(e, [h], halves[h])
+                prepare_block(1)
             if e >= SHIFT:
                 y = hid.tile([P, C], F32, name="y")
                 finish(e, 0, y[:])
 
         first = load(w1_v[LAST, 0])[0]
-        low, high = load(w1_v[LAST, 1][:, :, :PASS], w1_v[LAST, 1][:, :, PASS:])
+        low, high = load(w1_v[LAST, 1][:, :, :PASS], w1_v[LAST, 1][:, :, PASS:])[:2]
         *raw_w2, late_1, late_0 = load(
             *[w2_v[LAST, h] for h in range(HB)], gate_v[:, 1:, (LAST - 1) * C :], gate_v[:, :1, LAST * C :]
-        )
+        )[:4]
         gates[LAST - 1, 1], gates[LAST, 1], gates[LAST, 0] = late_1[:, 0, :C], late_1[:, 0, C:], late_0[:, 0, :]
         prepare_half(LAST, 0, 0, first[:, :, :PASS], LATE_START)
         prepare_half(LAST, 0, 1, first[:, :, PASS:], LATE_START)

@@ -162,8 +162,8 @@ def tile_routed_moe_kernel(tc, xT, w1, w2, gate, offs, out):
 
         def quantize_w2(grouped):
             width = grouped.shape[1] // PACK
-            codes = hid.tile([P, width], U32, name="w2_codes", bufs=5, align_bytes=64)
-            scales = hid.tile([P, width], U8, name="w2_scales", bufs=5, align_bytes=64)
+            codes = hid.tile([P, width], U32, name="w2_codes", bufs=6, align_bytes=64)
+            scales = hid.tile([P, width], U8, name="w2_scales", bufs=6, align_bytes=64)
             nc.vector.quantize_mx(out=codes[:].bitcast(FP8X4), scales=scales[:], in_=grouped)
             return [(codes[:, c0 : c0 + P], scales[:, c0 : c0 + P]) for c0 in range(0, width, P)]
 
@@ -265,15 +265,19 @@ def tile_routed_moe_kernel(tc, xT, w1, w2, gate, offs, out):
         blocks = [grp.tile([P, HB, P * PACK], BF16, name="grp_w2", bufs=2, align_bytes=64) for b in range(NB)]
         for h in range(HB):
             for b in range(NB):
-                copy = on_scalar if (h, b) == (0, 1) else on_vector
-                interleave(copy, blocks[b][:, h, :], raw_w2[h][:, :, b * P : (b + 1) * P])
+                if (h, b) == (0, 1):
+                    cut = P // 2
+                    interleave(on_vector, blocks[b][:, h, : cut * PACK], raw_w2[h][:, :, P : P + cut])
+                    interleave(on_scalar, blocks[b][:, h, cut * PACK :], raw_w2[h][:, :, P + cut :])
+                else:
+                    interleave(on_vector, blocks[b][:, h, :], raw_w2[h][:, :, b * P : (b + 1) * P])
         for h in range(HB):
             w2q[LAST, h, 0] = quantize_w2(blocks[0][:, h, :])[0]
         quantize_h(LAST, [1], halves[1])
-        for h, block in enumerate(quantize_w2(blocks[1][:].rearrange("p h c -> p (h c)"))):
-            w2q[LAST, h, 1] = block
+        for h in range(HB):
+            w2q[LAST, h, 1] = quantize_w2(blocks[1][:, h, :])[0]
 
-        finish(LAST - 1, 1, raw_w2[1][:, 0, P:])
+        finish(LAST - 1, 1, raw_w2[1][:, 0, :P])
         for b in range(NB):
             finish(LAST, b, raw_w2[0][:, b, :P])
             nc.sync.dma_start(out=out_v[b], in_=window[b][:])

from contextlib import ExitStack

import concourse.mybir as mybir

K, T, E, C, H, N = 1024, 768, 6, 128, 1024, 256
FLOPS = 2 * K * H * E * C + 2 * H * N * E * C

F32 = mybir.dt.float32
BF16 = mybir.dt.bfloat16
U32 = mybir.dt.uint32
U16 = mybir.dt.uint16
U8 = mybir.dt.uint8
FP8X4 = mybir.dt.float8_e4m3fn_x4
MULT = mybir.AluOpType.mult
SILU = mybir.ActivationFunctionType.Silu

P = 128
PACK = 4
PASS = P * PACK
G = K // PASS
HB = H // PASS
NB = N // P
LAST = E - 1
LIST_ROWS = 16
X_WIDE = 512
SHIFT = 2
GATHER = E * C // 2

NO_SCATTER = 80
LATE_START = 48
LAST_LOW = 96
LAST_HELP = 28


def tile_routed_moe_kernel(tc, xT, w1, w2, gate, offs, out):
    nc = tc.nc
    x_v = xT.rearrange("(g p j) t -> g p j t", p=P, j=PACK)
    w1_v = w1.rearrange("e (g p j) c -> e g p j c", p=P, j=PACK)
    w2_v = w2.rearrange("e (h p j) c -> e h p j c", p=P, j=PACK)
    gate_v = gate.rearrange("(b p) s -> p b s", p=P)
    out_v = out.rearrange("(b p) t -> b p t", p=P)
    on_vector, on_scalar = nc.vector.tensor_copy, nc.scalar.copy

    with ExitStack() as ctx:
        keep = ctx.enter_context(tc.tile_pool(name="keep", bufs=1))
        staging = ctx.enter_context(tc.tile_pool(name="staging", bufs=7))
        grp = ctx.enter_context(tc.tile_pool(name="grp", bufs=2))
        cod = ctx.enter_context(tc.tile_pool(name="cod", bufs=8))
        hid = ctx.enter_context(tc.tile_pool(name="hid", bufs=3))
        psum_a = ctx.enter_context(tc.psum_pool(name="psum_a", bufs=4))
        psum_y = ctx.enter_context(tc.psum_pool(name="psum_y", bufs=4))

        offsets = keep.tile([P, E * C // LIST_ROWS], U16, name="offsets")
        gate_sb = keep.tile([P, NB, LAST * C], F32, name="gate_sb", align_bytes=256)
        x_words = [keep.tile([P, T], U32, name=f"x_words{g}", align_bytes=64) for g in range(G)]
        x_scales = keep.tile([P, T], U8, name="x_scales", align_bytes=64)
        window = [keep.tile([P, T], F32, name=f"window{b}", align_bytes=256) for b in range(NB)]

        nc.gpsimd.memset(x_scales[:], 0)

        def load(*sources, at=0):
            slot = staging.tile([P, PACK * H], F32, name="slot", align_bytes=256)
            views = []
            for src in sources:
                size = src.shape[1] * src.shape[2]
                views.append(slot[:, at : at + size].rearrange("p (r c) -> p r c", r=src.shape[1]))
                nc.sync.dma_start(out=views[-1], in_=src)
                at += size
            return views + [slot]

        def interleave(copy, dst, rows):
            copy(
                out=dst.rearrange("p (c i u v) -> p c u i v", i=4, u=2, v=2),
                in_=rows.rearrange("p (u v) (c i) -> p c u i v", u=2, i=4),
            )

        def entries(first_slot, count):
            return offsets[:, first_slot // LIST_ROWS : (first_slot + count) // LIST_ROWS]

        raw_x = [load(x_v[g])[0] for g in range(G)]
        nc.sync.dma_start(offsets[:], offs)
        for g, copies in enumerate(((on_vector, on_scalar), (on_scalar, on_vector))):
            for (t0, t1), copy in zip(((0, X_WIDE), (X_WIDE, T)), copies):
                grouped = grp.tile([P, (t1 - t0) * PACK], BF16, name=f"grp_x{t0}", align_bytes=64)
                interleave(copy, grouped[:], raw_x[g][:, :, t0:t1])
                nc.vector.quantize_mx(
                    out=x_words[g][:, t0:t1].bitcast(FP8X4), scales=x_scales[PACK * g :, t0:t1], in_=grouped[:]
                )

        xq = {}
        w1q = {}
        w2q = {}
        hq = {}
        gates = {}

        slot_words = keep.tile([P, G, E * C], U32, name="slot_words", align_bytes=64)
        slot_scales = keep.tile([P, E * C], U8, name="slot_scales", align_bytes=64)
        for s0 in range(0, E * C, GATHER):
            for g in range(G):
                on_vector(out=slot_words[:, g, s0 : s0 + GATHER], in_=x_words[g][:].indirect(entries(s0, GATHER)))
            on_vector(out=slot_scales[:, s0 : s0 + GATHER], in_=x_scales[:].indirect(entries(s0, GATHER)))
        for e in range(E):
            for g in range(G):
                xq[e, g] = (slot_words[:, g, e * C : (e + 1) * C], slot_scales[PACK * g :, e * C : (e + 1) * C])

        def copy_w1(h, shares):
            grouped = grp.tile([P, PASS * PACK], BF16, name=f"grp_w1_{h}", bufs=3, align_bytes=64)
            dst = grouped[:].rearrange("p (t m u v) -> p m u t v", t=PACK, u=2, v=2)
            for rows, m0, t0, t1, copy in shares:
                src = rows.rearrange("p (u v) (m t) -> p m u t v", u=2, t=PACK)
                a, b = dst[:, m0 : m0 + src.shape[1], :, t0:t1, :], src[:, :, :, t0:t1, :]
                if t1 - t0 < PACK:
                    a, b = a.rearrange("p m u t v -> p m u v t"), b.rearrange("p m u t v -> p m u v t")
                copy(out=a, in_=b)
            return grouped

        def quantize_w1(e, g, h, grouped, cuts):
            codes = cod.tile([P, PASS], U32, name="w1_codes", align_bytes=64)
            scales = cod.tile([P, PASS], U8, name="w1_scales", align_bytes=64)
            for c0, c1 in zip(cuts, cuts[1:]):
                nc.vector.quantize_mx(
                    out=codes[:, c0:c1].bitcast(FP8X4),
                    scales=scales[:, c0:c1],
                    in_=grouped[:, c0 * PACK : c1 * PACK],
                )
            w1q[e, g, h] = (codes, scales)

        def prepare_half(e, g, h, rows, share, cuts=(0, PASS)):
            shares = [
                (0, share, on_vector),
                (share, P, on_scalar),
            ]
            shares = [(rows[:, :, m0 * PACK : m1 * PACK], m0, 0, PACK, copy) for m0, m1, copy in shares if m1 > m0]
            quantize_w1(e, g, h, copy_w1(h, shares), cuts)

        def layer1(e, h, grouped):
            acc = psum_a.tile([P, PACK, C], F32, name="acc_a")
            for g in range(G):
                codes, scales = w1q[e, g, h]
                for t in range(PACK):
                    nc.tensor.matmul_mx(
                        out=acc[:, t, :],
                        lhsT=codes[:, t * P : (t + 1) * P].bitcast(FP8X4),
                        lhsT_scale=scales[:, t * P : (t + 1) * P],
                        rhs=xq[e, g][0].bitcast(FP8X4),
                        rhs_scale=xq[e, g][1],
                        start=(g, t) == (0, 0),
                        stop=(g, t) == (G - 1, PACK - 1),
                    )
            nc.scalar.activation(
                grouped.rearrange("p (n t) -> p n t", t=PACK),
                acc[:].rearrange("p t n -> p n t"),
                SILU,
            )

        def quantize_h(e, hs, grouped):
            codes = hid.tile([P, len(hs) * C], U32, name="h_codes", bufs=5, align_bytes=64)
            scales = hid.tile([P, len(hs) * C], U8, name="h_scales", bufs=5, align_bytes=64)
            nc.vector.quantize_mx(out=codes[:].bitcast(FP8X4), scales=scales[:], in_=grouped)
            for i, h in enumerate(hs):
                hq[e, h] = (codes[:, i * C : (i + 1) * C], scales[:, i * C : (i + 1) * C])

        def quantize_w2(grouped):
            width = grouped.shape[1] // PACK
            codes = hid.tile([P, width], U32, name="w2_codes", bufs=6, align_bytes=64)
            scales = hid.tile([P, width], U8, name="w2_scales", bufs=6, align_bytes=64)
            nc.vector.quantize_mx(out=codes[:].bitcast(FP8X4), scales=scales[:], in_=grouped)
            return [(codes[:, c0 : c0 + P], scales[:, c0 : c0 + P]) for c0 in range(0, width, P)]

        def prepare_w2(e, passes):
            grouped = grp.tile([P, HB, N * PACK], BF16, name="grp_w2", bufs=2, align_bytes=64)
            for h, copy in enumerate((on_scalar, on_vector)):
                interleave(copy, grouped[:, h, :], passes[h])
            for i, block in enumerate(quantize_w2(grouped[:].rearrange("p h c -> p (h c)"))):
                w2q[e, i // NB, i % NB] = block

        def finish(e, b, room):
            acc = psum_y.tile([P, C], F32, name="acc_y")
            for h in range(HB):
                nc.tensor.matmul_mx(
                    out=acc[:],
                    lhsT=w2q[e, h, b][0].bitcast(FP8X4),
                    lhsT_scale=w2q[e, h, b][1],
                    rhs=hq[e, h][0].bitcast(FP8X4),
                    rhs_scale=hq[e, h][1],
                    start=(h == 0),
                    stop=(h == HB - 1),
                )
            nc.scalar.copy(out=room, in_=acc[:])
            nc.vector.tensor_tensor(window[b][:].indirect(entries(e * C, C)), room, gates[e, b], MULT)

        half = C * PACK
        for e in range(LAST):
            raw_w1 = [load(w1_v[e, g])[0] for g in range(G)]
            if e >= 2:
                *raw_w2, slot_w2 = load(*[w2_v[e, h] for h in range(HB)], at=P)
            else:
                both = load(w2[e].rearrange("(h p j) c -> p h (j c)", p=P, j=PACK))[0]
                raw_w2 = [both[:, h, :].rearrange("p (j c) -> p j c", j=PACK) for h in range(HB)]
            if e == 0:
                for b in range(NB):
                    early = LAST - b
                    nc.sync.dma_start(out=gate_sb[:, b, : early * C], in_=gate_v[:, b, : early * C])
                    for i in range(early):
                        gates[i, b] = gate_sb[:, b, i * C : (i + 1) * C]
            for g in range(G):
                low, high = raw_w1[g][:, :, :PASS], raw_w1[g][:, :, PASS:]
                scatter_here = 0 < e <= SHIFT or (e > SHIFT and g == 0)
                shares = (NO_SCATTER, NO_SCATTER) if (e, g) == (LAST - 1, 1) else (P, 0)
                prepare_half(e, g, 0, low, shares[0])
                if scatter_here:
                    finish(e - 1, g if e <= SHIFT else 1, low[:, 0, :C])
                prepare_half(e, g, 1, high, shares[1], (0, 2 * P, PASS) if (e, g) == (LAST - 1, 1) else (0, PASS))
            grouped_h = hid.tile([P, HB * half], BF16, name="grp_h", align_bytes=64)
            if e < LAST - 1:
                for h in range(HB):
                    layer1(e, h, grouped_h[:, h * half : (h + 1) * half])
                prepare_w2(e, raw_w2)
                quantize_h(e, range(HB), grouped_h[:])
            else:
                blocks = [grp.tile([P, HB, P * PACK], BF16, name="grp_w2", bufs=2, align_bytes=64) for b in range(NB)]

                def prepare_block(b):
                    for h, copy in enumerate((on_scalar, on_vector)):
                        interleave(copy, blocks[b][:, h, :], raw_w2[h][:, :, b * P : (b + 1) * P])
                    for h, block in enumerate(quantize_w2(blocks[b][:].rearrange("p h c -> p (h c)"))):
                        w2q[e, h, b] = block

                prepare_block(0)
                halves = (slot_w2[:, : half // 2].bitcast(BF16), grouped_h[:, half:])
                for h in range(HB):
                    layer1(e, h, halves[h])
                for h in range(HB):
                    quantize_h(e, [h], halves[h])
                prepare_block(1)
            if e >= SHIFT:
                y = hid.tile([P, C], F32, name="y")
                finish(e, 0, y[:])

        first = load(w1_v[LAST, 0])[0]
        low, high = load(w1_v[LAST, 1][:, :, :PASS], w1_v[LAST, 1][:, :, PASS:])[:2]
        *raw_w2, late_1, late_0 = load(
            *[w2_v[LAST, h] for h in range(HB)], gate_v[:, 1:, (LAST - 1) * C :], gate_v[:, :1, LAST * C :]
        )[:4]
        gates[LAST - 1, 1], gates[LAST, 1], gates[LAST, 0] = late_1[:, 0, :C], late_1[:, 0, C:], late_0[:, 0, :]
        prepare_half(LAST, 0, 0, first[:, :, :PASS], LATE_START)
        prepare_half(LAST, 0, 1, first[:, :, PASS:], LATE_START)
        prepare_half(LAST, 1, 0, low, LAST_LOW)
        pair = PACK // 2
        grouped = copy_w1(
            1,
            [
                (high, 0, 0, pair, on_vector),
                (high[:, :, : LAST_HELP * PACK], 0, pair, PACK, on_vector),
                (high[:, :, LAST_HELP * PACK :], LAST_HELP, pair, PACK, on_scalar),
            ],
        )
        quantize_w1(LAST, 1, 1, grouped, (0, 2 * P, 3 * P, PASS))
        last_h = hid.tile([P, half], BF16, name="grp_h", align_bytes=64)
        halves = (high[:, 0, PASS - half // 2 :].bitcast(BF16), last_h[:])
        for h in range(HB):
            layer1(LAST, h, halves[h])
        quantize_h(LAST, [0], halves[0])

        blocks = [grp.tile([P, HB, P * PACK], BF16, name="grp_w2", bufs=2, align_bytes=64) for b in range(NB)]
        for h in range(HB):
            for b in range(NB):
                if (h, b) == (0, 1):
                    cut = P // 2
                    interleave(on_vector, blocks[b][:, h, : cut * PACK], raw_w2[h][:, :, P : P + cut])
                    interleave(on_scalar, blocks[b][:, h, cut * PACK :], raw_w2[h][:, :, P + cut :])
                else:
                    interleave(on_vector, blocks[b][:, h, :], raw_w2[h][:, :, b * P : (b + 1) * P])
        for h in range(HB):
            w2q[LAST, h, 0] = quantize_w2(blocks[0][:, h, :])[0]
        quantize_h(LAST, [1], halves[1])
        for h in range(HB):
            w2q[LAST, h, 1] = quantize_w2(blocks[1][:, h, :])[0]

        finish(LAST - 1, 1, raw_w2[1][:, 0, :P])
        for b in range(NB):
            finish(LAST, b, raw_w2[0][:, b, :P])
            nc.sync.dma_start(out=out_v[b], in_=window[b][:])
